import numpy as np
import ml_dtypes


def mxq(x, axis, fmt="e4m3"):
    dtype, down = {"e4m3": (ml_dtypes.float8_e4m3fn, 7), "e5m2": (ml_dtypes.float8_e5m2, 14)}[fmt]
    v = np.moveaxis(np.asarray(x, np.float32).astype(ml_dtypes.bfloat16).astype(np.float64), axis, -1)
    blocks = v.reshape(v.shape[:-1] + (-1, 32))
    amax = np.abs(blocks).max(-1, keepdims=True)
    byte = np.maximum(np.where(amax > 0, np.frexp(amax)[1] - 1 + 127, 0) - down, 1)
    scale = np.exp2(byte - 127.0)
    codes = (blocks / scale).astype(np.float32).astype(dtype).astype(np.float64)
    return np.moveaxis((codes * scale).reshape(v.shape), -1, axis)


WIDE = False


def mx_kscale(k):
    if not WIDE:
        return np.ones(k)
    levels = np.array([24, -24, 12, -12, 0])
    if k % 512:
        return np.exp2(np.random.permutation(np.resize(levels, k // 32))).repeat(32)
    a = np.empty((k // 512, 16))
    for p in range(k // 512):
        a[p, :8] = np.random.permutation(np.resize(levels, 8))
        for g in range(8):
            far = levels[np.abs(levels - a[p, g]) >= 10]
            a[p, g + 8] = far[np.random.randint(len(far))]
    return np.exp2(a.ravel()).repeat(32)


def f64(x):
    return np.asarray(x).astype(np.float64)


def striped(idx):
    return np.tile(idx.reshape(-1, 16).T, (8, 1)).astype(np.uint16)


def unstriped(offs):
    return offs[:16].T.reshape(-1).astype(np.int64)


def striped8(idx):
    return np.concatenate([v.reshape(-1, 16).T for v in idx]).astype(np.uint16)


def unstriped8(offs):
    return np.stack([offs[16 * g:16 * g + 16].T.reshape(-1) for g in range(8)]).astype(np.int64)


E2M1 = np.array([0.0, 0.5, 1.0, 1.5, 2.0, 3.0, 4.0, 6.0, -0.0, -0.5, -1.0, -1.5, -2.0, -3.0, -4.0, -6.0])


def pack_weight(w, fmt):
    k, n = w.shape
    w = f64(np.asarray(w, np.float32).astype(ml_dtypes.bfloat16)).reshape(k // 32, 32, n)
    amax = np.abs(w).max(1)
    if fmt == "e4m3":
        byte = np.frexp(amax)[1] - 1 + 127 - 7
    else:
        mant, ex = np.frexp(amax / 6.0)
        byte = np.where(mant > 0.5, ex, ex - 1) + 127
    byte = np.clip(np.where(amax > 0, byte, 1), 1, 254)
    scaled = (w * np.exp2(127.0 - byte)[:, None, :]).reshape(k, n).astype(np.float32)
    by_word = np.ascontiguousarray(scaled.reshape(k // 512, 128, 4, n).transpose(0, 1, 3, 2))
    if fmt == "e4m3":
        words = by_word.astype(ml_dtypes.float8_e4m3fn).view(np.uint8)
    else:
        c = by_word.astype(ml_dtypes.float4_e2m1fn).view(np.uint8) & 0xF
        words = (c[..., 0::2] | (c[..., 1::2] << 4)).reshape(k // 512, 128, 2 * n)
    return np.ascontiguousarray(words), np.ascontiguousarray(byte.astype(np.uint8).reshape(k // 512, 16, n))


def unpack_weight(words, scales, fmt):
    g, _, n = scales.shape
    words = np.ascontiguousarray(words).reshape(g, 128, n, -1)
    if fmt == "e4m3":
        vals = words.view(ml_dtypes.float8_e4m3fn).astype(np.float64)
    else:
        nib = np.empty((g, 128, n, 4), np.uint8)
        nib[..., 0::2] = words & 0xF
        nib[..., 1::2] = words >> 4
        vals = E2M1[nib]
    vals = vals * np.repeat(np.exp2(scales.astype(np.float64) - 127.0), 8, axis=1)[..., None]
    return vals.transpose(0, 1, 3, 2).reshape(g * 512, n)


def planes(y):
    n, m = y.shape
    v = y.astype(np.float32).astype(ml_dtypes.bfloat16).astype(np.float64).reshape(n // 32, 32, m)
    top = np.abs(v).max(1)
    byte = np.clip(np.where(top > 0, np.frexp(top)[1] - 1 + 127 - 7, 1), 1, 254)
    codes = (v * np.exp2(127.0 - byte)[:, None, :]).reshape(n, m).astype(np.float32).astype(ml_dtypes.float8_e4m3fn).view(np.uint8)
    words = codes.reshape(n // 512, 128, 4, m).transpose(0, 1, 3, 2)
    return np.ascontiguousarray(words), np.ascontiguousarray(byte.astype(np.uint8).reshape(n // 512, 16, m))


def silu(f):
    return f / (1.0 + np.exp(-np.maximum(f, -700.0)))


K, L, R, N, T, J = 512, 512, 512, 512, 2048, 1024


def setup_inputs():
    n = np.random.standard_normal
    s = mx_kscale(K)[:, None]
    s2 = mx_kscale(L)[:, None]
    u = mx_kscale(R)[:, None]
    p_tab = pack_weight(n((L, T)) * s2, "e4m3")
    p_wa = pack_weight(n((K, R)) / np.sqrt(K) / s, "e2m1")
    p_wb = pack_weight(n((L, R)) / np.sqrt(L) / s2 * u.T, "e2m1")
    return {
        "tab_words": p_tab[0],
        "tab_scales": p_tab[1],
        "xT": (n((K, T)) * s).astype(np.float32),
        "wgt2": np.repeat(np.random.uniform(0.5, 2.0, (8, J)), 16, axis=0).astype(np.float32),
        "wa_words": p_wa[0],
        "wa_scales": p_wa[1],
        "wb_words": p_wb[0],
        "wb_scales": p_wb[1],
        "wd": (n((R, N)) / np.sqrt(R) / u).astype(np.float32),
        "offs": striped(np.random.permutation(T)[:J]),
        "offs2": striped8(np.stack([np.random.permutation(T)[:J] for _ in range(8)])),
    }


def reference(tab_words, tab_scales, xT, wgt2, wa_words, wa_scales, wb_words, wb_scales, wd, offs, offs2):
    idx = unstriped(offs)
    idx2 = unstriped8(offs2)
    tab_ = unpack_weight(tab_words, tab_scales, "e4m3")[:, idx]
    rows = np.arange(K)
    xg = f64(wgt2)[rows // 4 % 128] * f64(xT)[rows[:, None], idx2[rows % 512 // 64]]
    xT_ = mxq(xg, 0, "e4m3")
    wa_ = unpack_weight(wa_words, wa_scales, "e2m1")
    wb_ = unpack_weight(wb_words, wb_scales, "e2m1")
    ya = wa_.T @ xT_
    yb = wb_.T @ tab_
    h = silu(ya) * yb
    h_ = mxq(h, 0, "e4m3")
    wd_ = mxq(f64(wd), 0, "e4m3")
    y = wd_.T @ h_
    return (y,) + planes(y)

@@ -1,0 +1,204 @@
+from contextlib import ExitStack
+
+import concourse.mybir as mybir
+
+K, L, R, N, T, J = 512, 512, 512, 512, 2048, 1024
+FLOPS = 2 * J * (K * R + L * R + R * N)
+
+F32 = mybir.dt.float32
+BF16 = mybir.dt.bfloat16
+I32 = mybir.dt.int32
+U32 = mybir.dt.uint32
+U16 = mybir.dt.uint16
+U8 = mybir.dt.uint8
+FP8X4 = mybir.dt.float8_e4m3fn_x4
+FP4X4 = mybir.dt.float4_e2m1fn_x4
+MULT = mybir.AluOpType.mult
+SILU = mybir.ActivationFunctionType.Silu
+
+P = 128
+PACK = 4
+GW = 256
+CW = 128
+VECTOR_CASTS_FROM = 5
+
+
+def tile_list_htabg_glu_noneP_kernel(
+    tc, tab_words, tab_scales, xT, wgt2, wa_words, wa_scales, wb_words, wb_scales, wd, offs, offs2,
+    out_0, out_1, out_2,
+):
+    nc = tc.nc
+    groups = J // GW
+    chunks = J // CW
+    with ExitStack() as ctx:
+        keep = ctx.enter_context(tc.tile_pool(name="keep", bufs=1))
+        ring = ctx.enter_context(tc.tile_pool(name="ring", bufs=3))
+        psum = ctx.enter_context(tc.psum_pool(name="psum", bufs=1))
+
+        head_list = keep.tile([P, J // 16], U16, name="head_list")
+        tab_list = keep.tile([P, J // 16], U16, name="tab_list")
+        tab_sc = keep.tile([P, T], U8, name="tab_sc", align_bytes=64)
+        w_sc_raw = keep.tile([P, 2 * R], U8, name="w_sc_raw", align_bytes=64)
+        nc.gpsimd.memset(tab_sc[:].bitcast(I32), 0)
+        nc.vector.memset(w_sc_raw[:].bitcast(I32), 0)
+
+        warm_in = keep.tile([P, 1], F32, name="warm_in")
+        warm_out = keep.tile([P, 1], F32, name="warm_out")
+        nc.vector.memset(warm_in[:], 0.0)
+        nc.scalar.activation(warm_out[:], warm_in[:], SILU)
+
+        nc.sync.dma_start(head_list[:], offs2)
+        nc.sync.dma_start(tab_list[:], offs)
+        wgt_first = keep.tile([P, GW], F32, name="wgt_first")
+        wgt_rest = keep.tile([P, J - GW], F32, name="wgt_rest")
+        x_rows = xT.rearrange("(p i) t -> p i t", i=PACK)
+        x_planes = [keep.tile([P, T], F32, name="x_plane%d" % i) for i in range(PACK)]
+        nc.sync.dma_start(wgt_first[:], wgt2[:, 0:GW])
+        for q in range(4):
+            nc.sync.dma_start(tab_sc[32 * q : 32 * q + 4, :].bitcast(I32), tab_scales[0, 4 * q : 4 * q + 4, :].bitcast(I32))
+        nc.sync.dma_start(x_planes[0][:], x_rows[:, 0, :])
+        nc.sync.dma_start(wgt_rest[:], wgt2[:, GW:J])
+        for i in range(1, PACK):
+            nc.sync.dma_start(x_planes[i][:], x_rows[:, i, :])
+
+        w_raw = [keep.tile([P, 2 * R], U8, name="w_raw%d" % a) for a in range(2)]
+        for a, (words, scales) in enumerate(((wa_words, wa_scales), (wb_words, wb_scales))):
+            nc.sync.dma_start(w_raw[a][:].bitcast(I32), words[0].bitcast(I32))
+            for q in range(4):
+                nc.sync.dma_start(
+                    w_sc_raw[32 * q : 32 * q + 4, a * R : (a + 1) * R].bitcast(I32),
+                    scales[0, 4 * q : 4 * q + 4, :].bitcast(I32),
+                )
+        wd_raw = keep.tile([P, PACK, N], F32, name="wd_raw")
+        wd_rows = wd.rearrange("(b t i) n -> i b t n", t=PACK, i=8)
+        for i in range(8):
+            nc.sync.dma_start(wd_raw[i:P:8, :, :], wd_rows[i])
+        tab_w = keep.tile([P, T], I32, name="tab_w")
+        nc.sync.dma_start(tab_w[:], tab_words[0].rearrange("p t i -> p (t i)").bitcast(I32))
+
+        v_sc = keep.tile([P, J], U8, name="v_sc", align_bytes=64)
+        nc.vector.tensor_copy(v_sc[:], tab_sc[:].indirect(tab_list[:]))
+
+        picked = [keep.tile([P, PACK, GW], F32, name="picked%d" % g) for g in range(groups)]
+
+        def pick(i, g):
+            wgt = wgt_first[:] if g == 0 else wgt_rest[:, (g - 1) * GW : g * GW]
+            cols = slice(g * GW // 16, (g + 1) * GW // 16)
+            nc.vector.tensor_tensor(picked[g][:, i, :], x_planes[i][:].indirect(head_list[:, cols]), wgt, MULT)
+
+        for i in range(PACK - 1):
+            for g in range(groups):
+                pick(i, g)
+
+        w_sc = keep.tile([P, 2 * R], U8, name="w_sc", align_bytes=64)
+        nc.vector.tensor_copy(
+            w_sc[:].bitcast(I32).rearrange("p (a t b w) -> p a t b w", a=2, t=PACK, w=2),
+            w_sc_raw[:].bitcast(I32).rearrange("p (a b t w) -> p a t b w", a=2, t=PACK, w=2),
+        )
+        w_codes = [keep.tile([P, 2 * R], U8, name="w_codes%d" % a, align_bytes=64) for a in range(2)]
+
+        def deal_words(a):
+            nc.vector.tensor_copy(
+                w_codes[a][:].bitcast(I32).rearrange("p (t b w) -> p t b w", t=PACK, w=4),
+                w_raw[a][:].bitcast(I32).rearrange("p (b t w) -> p t b w", t=PACK, w=4),
+            )
+
+        x_codes = [keep.tile([P, GW], U32, name="x_codes%d" % g, align_bytes=64) for g in range(groups)]
+        x_sc = [keep.tile([P, GW], U8, name="x_sc%d" % g, align_bytes=64) for g in range(groups)]
+        v_codes = [keep.tile([P, GW], U32, name="v_codes%d" % g, align_bytes=64) for g in range(groups)]
+        wd_codes = keep.tile([P, N], U32, name="wd_codes", align_bytes=64)
+        wd_sc = keep.tile([P, N], U8, name="wd_sc", align_bytes=64)
+        y_codes = [keep.tile([P, GW], I32, name="y_codes%d" % g, align_bytes=64) for g in range(groups)]
+        y_sc = keep.tile([P, J], U8, name="y_sc", align_bytes=64)
+        y_f32 = [keep.tile([P, PACK, CW], F32, name="y_f32_%d" % c) for c in range(chunks)]
+        h_codes = [keep.tile([P, CW], U32, name="h_codes%d" % c, align_bytes=64) for c in range(chunks)]
+        h_sc = [keep.tile([P, CW], U8, name="h_sc%d" % c, align_bytes=64) for c in range(chunks)]
+        out_rows = out_0.rearrange("(p t) j -> p t j", t=PACK)
+        out_words = out_1[0].rearrange("p j i -> p (j i)").bitcast(I32)
+
+        def prepare(g):
+            pick(PACK - 1, g)
+            x_bf = ring.tile([P, GW * PACK], BF16, name="x_bf", align_bytes=64)
+            nc.scalar.copy(
+                x_bf[:].rearrange("p (c i t) -> p c t i", i=4, t=PACK),
+                picked[g][:].rearrange("p t (c i) -> p c t i", i=4),
+            )
+            nc.vector.quantize_mx(x_codes[g][:].bitcast(FP8X4), x_sc[g][:], x_bf[:])
+            cols = slice(g * GW // 16, (g + 1) * GW // 16)
+            nc.vector.tensor_copy(v_codes[g][:], tab_w[:].bitcast(U32).indirect(tab_list[:, cols]))
+
+        def product(bank, a, codes, scales):
+            for t in range(PACK):
+                nc.tensor.matmul_mx(
+                    bank[:, t, :],
+                    lhsT=w_codes[a][:, 2 * P * t : 2 * P * (t + 1)].bitcast(FP4X4),
+                    lhsT_scale=w_sc[:, a * R + P * t : a * R + P * (t + 1)],
+                    rhs=codes.bitcast(FP8X4),
+                    rhs_scale=scales,
+                    start=True,
+                    stop=True,
+                )
+
+        def first_layer(c):
+            g, cols = divmod(c * CW, GW)[0], slice(c * CW % GW, c * CW % GW + CW)
+            ya = psum.tile([P, PACK, CW], F32, name="ya", bufs=2)
+            yb = psum.tile([P, PACK, CW], F32, name="yb", bufs=3)
+            product(ya, 0, x_codes[g][:, cols], x_sc[g][:, cols])
+            product(yb, 1, v_codes[g][:, cols], v_sc[:, c * CW : (c + 1) * CW])
+            gate = ring.tile([P, CW, PACK], F32, name="gate", bufs=chunks)
+            nc.scalar.activation(gate[:], ya[:].rearrange("p t j -> p j t"), SILU)
+            h_bf = ring.tile([P, CW, PACK], BF16, name="h_bf", align_bytes=64)
+            nc.vector.tensor_tensor(h_bf[:], yb[:].rearrange("p t j -> p j t"), gate[:], MULT)
+            nc.vector.quantize_mx(h_codes[c][:].bitcast(FP8X4), h_sc[c][:], h_bf[:].rearrange("p j t -> p (j t)"))
+
+        def quantise_wd():
+            wd_bf = keep.tile([P, N * PACK], BF16, name="wd_bf", align_bytes=64)
+            nc.vector.tensor_copy(
+                wd_bf[:].rearrange("p (u m t) -> p m t u", u=PACK, t=PACK),
+                wd_raw[:].rearrange("p t (m u) -> p m t u", u=PACK),
+            )
+            nc.vector.quantize_mx(wd_codes[:].bitcast(FP8X4), wd_sc[:], wd_bf[:])
+
+        def second_layer(c):
+            g, cols = divmod(c * CW, GW)[0], slice(c * CW % GW, c * CW % GW + CW)
+            y = psum.tile([P, PACK, CW], F32, name="y", bufs=3)
+            for u in range(PACK):
+                nc.tensor.matmul_mx(
+                    y[:, u, :],
+                    lhsT=wd_codes[:, P * u : P * (u + 1)].bitcast(FP8X4),
+                    lhsT_scale=wd_sc[:, P * u : P * (u + 1)],
+                    rhs=h_codes[c][:].bitcast(FP8X4),
+                    rhs_scale=h_sc[c][:],
+                    start=True,
+                    stop=True,
+                )
+            nc.scalar.copy(y_f32[c][:], y[:])
+            nc.sync.dma_start(out_rows[:, :, c * CW : (c + 1) * CW], y_f32[c][:])
+            y_bf = ring.tile([P, CW * PACK], BF16, name="y_bf", align_bytes=64)
+            if c < VECTOR_CASTS_FROM:
+                nc.scalar.copy(y_bf[:].rearrange("p (j t) -> p j t", t=PACK), y[:].rearrange("p t j -> p j t"))
+            else:
+                nc.vector.tensor_copy(
+                    y_bf[:].rearrange("p (c i t) -> p c t i", i=4, t=PACK),
+                    y_f32[c][:].rearrange("p t (c i) -> p c t i", i=4),
+                )
+            nc.vector.quantize_mx(y_codes[g][:, cols].bitcast(FP8X4), y_sc[:, c * CW : (c + 1) * CW], y_bf[:])
+            if (c + 1) * CW % GW == 0:
+                nc.sync.dma_start(out_words[:, g * GW : (g + 1) * GW], y_codes[g][:])
+
+        deal_words(0)
+        prepare(0)
+        deal_words(1)
+        prepare(1)
+        quantise_wd()
+        first_layer(0)
+        first_layer(1)
+        for c in range(2, chunks + 2):
+            if c % 2 == 0 and c // 2 + 1 < groups:
+                prepare(c // 2 + 1)
+            if c < chunks:
+                first_layer(c)
+            second_layer(c - 2)
+        for q in range(4):
+            queue = nc.sync if q % 2 == 0 else nc.scalar
+            queue.dma_start(out_2[0, 4 * q : 4 * q + 4, :].bitcast(I32), y_sc[32 * q : 32 * q + 4, :].bitcast(I32))

@@ -20,7 +20,7 @@ P = 128
 PACK = 4
 GW = 256
 CW = 128
-VECTOR_CASTS_FROM = 5
+VECTOR_CASTS_FROM = 4
 
 
 def tile_list_htabg_glu_noneP_kernel(
@@ -49,46 +49,55 @@ def tile_list_htabg_glu_noneP_kernel(
 
         nc.sync.dma_start(head_list[:], offs2)
         nc.sync.dma_start(tab_list[:], offs)
-        wgt_first = keep.tile([P, GW], F32, name="wgt_first")
-        wgt_rest = keep.tile([P, J - GW], F32, name="wgt_rest")
+        wgt = keep.tile([P, J], F32, name="wgt")
         x_rows = xT.rearrange("(p i) t -> p i t", i=PACK)
         x_planes = [keep.tile([P, T], F32, name="x_plane%d" % i) for i in range(PACK)]
-        nc.sync.dma_start(wgt_first[:], wgt2[:, 0:GW])
         for q in range(4):
             nc.sync.dma_start(tab_sc[32 * q : 32 * q + 4, :].bitcast(I32), tab_scales[0, 4 * q : 4 * q + 4, :].bitcast(I32))
+        nc.sync.dma_start(wgt[:], wgt2)
         nc.sync.dma_start(x_planes[0][:], x_rows[:, 0, :])
-        nc.sync.dma_start(wgt_rest[:], wgt2[:, GW:J])
-        for i in range(1, PACK):
-            nc.sync.dma_start(x_planes[i][:], x_rows[:, i, :])
-
-        w_raw = [keep.tile([P, 2 * R], U8, name="w_raw%d" % a) for a in range(2)]
-        for a, (words, scales) in enumerate(((wa_words, wa_scales), (wb_words, wb_scales))):
-            nc.sync.dma_start(w_raw[a][:].bitcast(I32), words[0].bitcast(I32))
+        tab_w = keep.tile([P, T], I32, name="tab_w")
+        for a, scales in enumerate((wa_scales, wb_scales)):
+            if a == 0:
+                nc.sync.dma_start(x_planes[1][:], x_rows[:, 1, :])
+            else:
+                nc.sync.dma_start(tab_w[:], tab_words[0].rearrange("p t i -> p (t i)").bitcast(I32))
             for q in range(4):
                 nc.sync.dma_start(
                     w_sc_raw[32 * q : 32 * q + 4, a * R : (a + 1) * R].bitcast(I32),
                     scales[0, 4 * q : 4 * q + 4, :].bitcast(I32),
                 )
+        w_raw = [keep.tile([P, 2 * R], U8, name="w_raw%d" % a) for a in range(2)]
+        for a, words in enumerate((wa_words, wb_words)):
+            nc.sync.dma_start(w_raw[a][:].bitcast(I32), words[0].bitcast(I32))
+        nc.sync.dma_start(x_planes[2][:], x_rows[:, 2, :])
+        nc.sync.dma_start(x_planes[3][:], x_rows[:, 3, :])
         wd_raw = keep.tile([P, PACK, N], F32, name="wd_raw")
-        wd_rows = wd.rearrange("(b t i) n -> i b t n", t=PACK, i=8)
-        for i in range(8):
-            nc.sync.dma_start(wd_raw[i:P:8, :, :], wd_rows[i])
-        tab_w = keep.tile([P, T], I32, name="tab_w")
-        nc.sync.dma_start(tab_w[:], tab_words[0].rearrange("p t i -> p (t i)").bitcast(I32))
+        wd_rows = wd.rearrange("(b t i) n -> t b i n", t=PACK, i=8)
+        for t in range(PACK):
+            nc.sync.dma_start(wd_raw[:, t, :], wd_rows[t])
 
         v_sc = keep.tile([P, J], U8, name="v_sc", align_bytes=64)
         nc.vector.tensor_copy(v_sc[:], tab_sc[:].indirect(tab_list[:]))
 
-        picked = [keep.tile([P, PACK, GW], F32, name="picked%d" % g) for g in range(groups)]
+        x_bf = [keep.tile([P, GW, PACK], BF16, name="x_bf%d" % g, align_bytes=64) for g in range(groups)]
+        picked_lo = keep.tile([P, 2, J], F32, name="picked_lo")
+        picked_hi = [keep.tile([P, 2, GW], F32, name="picked_hi%d" % g) for g in range(groups)]
+        for i in range(2):
+            nc.vector.tensor_tensor(picked_lo[:, i, :], x_planes[i][:].indirect(head_list[:]), wgt[:], MULT)
+        for g in range(groups):
+            nc.scalar.copy(x_bf[g][:, :, 0:2], picked_lo[:, :, g * GW : (g + 1) * GW].rearrange("p t j -> p j t"))
+        v_codes = keep.tile([P, J], U32, name="v_codes", align_bytes=64)
+        nc.vector.tensor_copy(v_codes[:], tab_w[:].bitcast(U32).indirect(tab_list[:]))
 
         def pick(i, g):
-            wgt = wgt_first[:] if g == 0 else wgt_rest[:, (g - 1) * GW : g * GW]
             cols = slice(g * GW // 16, (g + 1) * GW // 16)
-            nc.vector.tensor_tensor(picked[g][:, i, :], x_planes[i][:].indirect(head_list[:, cols]), wgt, MULT)
+            nc.vector.tensor_tensor(
+                picked_hi[g][:, i - 2, :], x_planes[i][:].indirect(head_list[:, cols]), wgt[:, g * GW : (g + 1) * GW], MULT
+            )
 
-        for i in range(PACK - 1):
-            for g in range(groups):
-                pick(i, g)
+        for g in range(groups):
+            pick(2, g)
 
         w_sc = keep.tile([P, 2 * R], U8, name="w_sc", align_bytes=64)
         nc.vector.tensor_copy(
@@ -105,12 +114,13 @@ def tile_list_htabg_glu_noneP_kernel(
 
         x_codes = [keep.tile([P, GW], U32, name="x_codes%d" % g, align_bytes=64) for g in range(groups)]
         x_sc = [keep.tile([P, GW], U8, name="x_sc%d" % g, align_bytes=64) for g in range(groups)]
-        v_codes = [keep.tile([P, GW], U32, name="v_codes%d" % g, align_bytes=64) for g in range(groups)]
         wd_codes = keep.tile([P, N], U32, name="wd_codes", align_bytes=64)
         wd_sc = keep.tile([P, N], U8, name="wd_sc", align_bytes=64)
         y_codes = [keep.tile([P, GW], I32, name="y_codes%d" % g, align_bytes=64) for g in range(groups)]
         y_sc = keep.tile([P, J], U8, name="y_sc", align_bytes=64)
-        y_f32 = [keep.tile([P, PACK, CW], F32, name="y_f32_%d" % c) for c in range(chunks)]
+        y_f32 = [keep.tile([P, PACK, GW], F32, name="y_f32_%d" % g) for g in range(groups - 1)]
+        y_last = [keep.tile([P, PACK, CW], F32, name="y_last%d" % e) for e in range(2)]
+        y_bf = [keep.tile([P, GW, PACK], BF16, name="y_bf%d" % g, align_bytes=64) for g in range(groups)]
         h_codes = [keep.tile([P, CW], U32, name="h_codes%d" % c, align_bytes=64) for c in range(chunks)]
         h_sc = [keep.tile([P, CW], U8, name="h_sc%d" % c, align_bytes=64) for c in range(chunks)]
         out_rows = out_0.rearrange("(p t) j -> p t j", t=PACK)
@@ -118,14 +128,8 @@ def tile_list_htabg_glu_noneP_kernel(
 
         def prepare(g):
             pick(PACK - 1, g)
-            x_bf = ring.tile([P, GW * PACK], BF16, name="x_bf", align_bytes=64)
-            nc.scalar.copy(
-                x_bf[:].rearrange("p (c i t) -> p c t i", i=4, t=PACK),
-                picked[g][:].rearrange("p t (c i) -> p c t i", i=4),
-            )
-            nc.vector.quantize_mx(x_codes[g][:].bitcast(FP8X4), x_sc[g][:], x_bf[:])
-            cols = slice(g * GW // 16, (g + 1) * GW // 16)
-            nc.vector.tensor_copy(v_codes[g][:], tab_w[:].bitcast(U32).indirect(tab_list[:, cols]))
+            nc.scalar.copy(x_bf[g][:, :, 2:4], picked_hi[g][:].rearrange("p t j -> p j t"))
+            nc.vector.quantize_mx(x_codes[g][:].bitcast(FP8X4), x_sc[g][:], x_bf[g][:].rearrange("p j t -> p (j t)"))
 
         def product(bank, a, codes, scales):
             for t in range(PACK):
@@ -144,7 +148,7 @@ def tile_list_htabg_glu_noneP_kernel(
             ya = psum.tile([P, PACK, CW], F32, name="ya", bufs=2)
             yb = psum.tile([P, PACK, CW], F32, name="yb", bufs=3)
             product(ya, 0, x_codes[g][:, cols], x_sc[g][:, cols])
-            product(yb, 1, v_codes[g][:, cols], v_sc[:, c * CW : (c + 1) * CW])
+            product(yb, 1, v_codes[:, c * CW : (c + 1) * CW], v_sc[:, c * CW : (c + 1) * CW])
             gate = ring.tile([P, CW, PACK], F32, name="gate", bufs=chunks)
             nc.scalar.activation(gate[:], ya[:].rearrange("p t j -> p j t"), SILU)
             h_bf = ring.tile([P, CW, PACK], BF16, name="h_bf", align_bytes=64)
@@ -154,8 +158,8 @@ def tile_list_htabg_glu_noneP_kernel(
         def quantise_wd():
             wd_bf = keep.tile([P, N * PACK], BF16, name="wd_bf", align_bytes=64)
             nc.vector.tensor_copy(
-                wd_bf[:].rearrange("p (u m t) -> p m t u", u=PACK, t=PACK),
-                wd_raw[:].rearrange("p t (m u) -> p m t u", u=PACK),
+                wd_bf[:].rearrange("p (u m t) -> p m u t", u=PACK, t=PACK),
+                wd_raw[:].rearrange("p t (m u) -> p m u t", u=PACK),
             )
             nc.vector.quantize_mx(wd_codes[:].bitcast(FP8X4), wd_sc[:], wd_bf[:])
 
@@ -172,19 +176,27 @@ def tile_list_htabg_glu_noneP_kernel(
                     start=True,
                     stop=True,
                 )
-            nc.scalar.copy(y_f32[c][:], y[:])
-            nc.sync.dma_start(out_rows[:, :, c * CW : (c + 1) * CW], y_f32[c][:])
-            y_bf = ring.tile([P, CW * PACK], BF16, name="y_bf", align_bytes=64)
+            last = g == groups - 1
+            staged = y_last[c % 2][:] if last else y_f32[g][:, :, cols]
+            nc.scalar.copy(staged, y[:])
             if c < VECTOR_CASTS_FROM:
-                nc.scalar.copy(y_bf[:].rearrange("p (j t) -> p j t", t=PACK), y[:].rearrange("p t j -> p j t"))
-            else:
+                nc.scalar.copy(y_bf[g][:, cols, :], y[:].rearrange("p t j -> p j t"))
+            if last:
+                hand_out(g, cols, staged)
+            elif c % 2 == 1:
+                hand_out(g, slice(0, GW), y_f32[g][:])
+
+        def hand_out(g, cols, staged):
+            places = slice(g * GW + cols.start, g * GW + cols.stop)
+            nc.sync.dma_start(out_rows[:, :, places], staged)
+            rounded = y_bf[g][:, cols, :].rearrange("p j t -> p (j t)")
+            if places.start >= VECTOR_CASTS_FROM * CW:
                 nc.vector.tensor_copy(
-                    y_bf[:].rearrange("p (c i t) -> p c t i", i=4, t=PACK),
-                    y_f32[c][:].rearrange("p t (c i) -> p c t i", i=4),
+                    rounded.rearrange("p (c i t) -> p c t i", i=4, t=PACK),
+                    staged.rearrange("p t (c i) -> p c t i", i=4),
                 )
-            nc.vector.quantize_mx(y_codes[g][:, cols].bitcast(FP8X4), y_sc[:, c * CW : (c + 1) * CW], y_bf[:])
-            if (c + 1) * CW % GW == 0:
-                nc.sync.dma_start(out_words[:, g * GW : (g + 1) * GW], y_codes[g][:])
+            nc.vector.quantize_mx(y_codes[g][:, cols].bitcast(FP8X4), y_sc[:, places], rounded)
+            nc.sync.dma_start(out_words[:, places], y_codes[g][:, cols])
 
         deal_words(0)
         prepare(0)

@@ -50,11 +50,11 @@ def tile_list_htabg_glu_noneP_kernel(
         nc.sync.dma_start(head_list[:], offs2)
         nc.sync.dma_start(tab_list[:], offs)
         wgt = keep.tile([P, J], F32, name="wgt")
+        nc.sync.dma_start(wgt[:], wgt2)
         x_rows = xT.rearrange("(p i) t -> p i t", i=PACK)
         x_planes = [keep.tile([P, T], F32, name="x_plane%d" % i) for i in range(PACK)]
         for q in range(4):
-            nc.sync.dma_start(tab_sc[32 * q : 32 * q + 4, :].bitcast(I32), tab_scales[0, 4 * q : 4 * q + 4, :].bitcast(I32))
-        nc.sync.dma_start(wgt[:], wgt2)
+            nc.sync.dma_start(tab_sc[q:P:32, :].bitcast(I32), tab_scales[0, q:16:4, :].bitcast(I32))
         nc.sync.dma_start(x_planes[0][:], x_rows[:, 0, :])
         tab_w = keep.tile([P, T], I32, name="tab_w")
         for a, scales in enumerate((wa_scales, wb_scales)):
@@ -64,12 +64,12 @@ def tile_list_htabg_glu_noneP_kernel(
                 nc.sync.dma_start(tab_w[:], tab_words[0].rearrange("p t i -> p (t i)").bitcast(I32))
             for q in range(4):
                 nc.sync.dma_start(
-                    w_sc_raw[32 * q : 32 * q + 4, a * R : (a + 1) * R].bitcast(I32),
-                    scales[0, 4 * q : 4 * q + 4, :].bitcast(I32),
+                    w_sc_raw[q:P:32, a * R : (a + 1) * R].bitcast(I32),
+                    scales[0, q:16:4, :].bitcast(I32),
                 )
-        w_raw = [keep.tile([P, 2 * R], U8, name="w_raw%d" % a) for a in range(2)]
+        w_raw = keep.tile([P, 2, 2 * R], U8, name="w_raw")
         for a, words in enumerate((wa_words, wb_words)):
-            nc.sync.dma_start(w_raw[a][:].bitcast(I32), words[0].bitcast(I32))
+            nc.sync.dma_start(w_raw[:, a, :].bitcast(I32), words[0].bitcast(I32))
         nc.sync.dma_start(x_planes[2][:], x_rows[:, 2, :])
         nc.sync.dma_start(x_planes[3][:], x_rows[:, 3, :])
         wd_raw = keep.tile([P, PACK, N], F32, name="wd_raw")
@@ -82,7 +82,7 @@ def tile_list_htabg_glu_noneP_kernel(
 
         x_bf = [keep.tile([P, GW, PACK], BF16, name="x_bf%d" % g, align_bytes=64) for g in range(groups)]
         picked_lo = keep.tile([P, 2, J], F32, name="picked_lo")
-        picked_hi = [keep.tile([P, 2, GW], F32, name="picked_hi%d" % g) for g in range(groups)]
+        picked_hi = keep.tile([P, 2, J], F32, name="picked_hi")
         for i in range(2):
             nc.vector.tensor_tensor(picked_lo[:, i, :], x_planes[i][:].indirect(head_list[:]), wgt[:], MULT)
         for g in range(groups):
@@ -90,26 +90,19 @@ def tile_list_htabg_glu_noneP_kernel(
         v_codes = keep.tile([P, J], U32, name="v_codes", align_bytes=64)
         nc.vector.tensor_copy(v_codes[:], tab_w[:].bitcast(U32).indirect(tab_list[:]))
 
-        def pick(i, g):
-            cols = slice(g * GW // 16, (g + 1) * GW // 16)
-            nc.vector.tensor_tensor(
-                picked_hi[g][:, i - 2, :], x_planes[i][:].indirect(head_list[:, cols]), wgt[:, g * GW : (g + 1) * GW], MULT
-            )
-
-        for g in range(groups):
-            pick(2, g)
+        nc.vector.tensor_tensor(picked_hi[:, 0, :], x_planes[2][:].indirect(head_list[:]), wgt[:], MULT)
 
         w_sc = keep.tile([P, 2 * R], U8, name="w_sc", align_bytes=64)
         nc.vector.tensor_copy(
             w_sc[:].bitcast(I32).rearrange("p (a t b w) -> p a t b w", a=2, t=PACK, w=2),
             w_sc_raw[:].bitcast(I32).rearrange("p (a b t w) -> p a t b w", a=2, t=PACK, w=2),
         )
-        w_codes = [keep.tile([P, 2 * R], U8, name="w_codes%d" % a, align_bytes=64) for a in range(2)]
+        w_codes = keep.tile([P, 2, 2 * R], U8, name="w_codes", align_bytes=64)
 
-        def deal_words(a):
+        def deal_words():
             nc.vector.tensor_copy(
-                w_codes[a][:].bitcast(I32).rearrange("p (t b w) -> p t b w", t=PACK, w=4),
-                w_raw[a][:].bitcast(I32).rearrange("p (b t w) -> p t b w", t=PACK, w=4),
+                w_codes[:].bitcast(I32).rearrange("p a (t b w) -> p a t b w", t=PACK, w=4),
+                w_raw[:].bitcast(I32).rearrange("p a (b t w) -> p a t b w", t=PACK, w=4),
             )
 
         x_codes = [keep.tile([P, GW], U32, name="x_codes%d" % g, align_bytes=64) for g in range(groups)]
@@ -127,15 +120,18 @@ def tile_list_htabg_glu_noneP_kernel(
         out_words = out_1[0].rearrange("p j i -> p (j i)").bitcast(I32)
 
         def prepare(g):
-            pick(PACK - 1, g)
-            nc.scalar.copy(x_bf[g][:, :, 2:4], picked_hi[g][:].rearrange("p t j -> p j t"))
+            cols = slice(g * GW, (g + 1) * GW)
+            nc.vector.tensor_tensor(
+                picked_hi[:, 1, cols], x_planes[3][:].indirect(head_list[:, g * GW // 16 : (g + 1) * GW // 16]), wgt[:, cols], MULT
+            )
+            nc.scalar.copy(x_bf[g][:, :, 2:4], picked_hi[:, :, cols].rearrange("p t j -> p j t"))
             nc.vector.quantize_mx(x_codes[g][:].bitcast(FP8X4), x_sc[g][:], x_bf[g][:].rearrange("p j t -> p (j t)"))
 
         def product(bank, a, codes, scales):
             for t in range(PACK):
                 nc.tensor.matmul_mx(
                     bank[:, t, :],
-                    lhsT=w_codes[a][:, 2 * P * t : 2 * P * (t + 1)].bitcast(FP4X4),
+                    lhsT=w_codes[:, a, 2 * P * t : 2 * P * (t + 1)].bitcast(FP4X4),
                     lhsT_scale=w_sc[:, a * R + P * t : a * R + P * (t + 1)],
                     rhs=codes.bitcast(FP8X4),
                     rhs_scale=scales,
@@ -196,11 +192,13 @@ def tile_list_htabg_glu_noneP_kernel(
                     staged.rearrange("p t (c i) -> p c t i", i=4),
                 )
             nc.vector.quantize_mx(y_codes[g][:, cols].bitcast(FP8X4), y_sc[:, places], rounded)
-            nc.sync.dma_start(out_words[:, places], y_codes[g][:, cols])
+            if cols.stop == GW:
+                nc.scalar.dma_start(out_words[:, g * GW : (g + 1) * GW], y_codes[g][:]) if g == groups - 1 else nc.sync.dma_start(
+                    out_words[:, g * GW : (g + 1) * GW], y_codes[g][:]
+                )
 
-        deal_words(0)
+        deal_words()
         prepare(0)
-        deal_words(1)
         prepare(1)
         quantise_wd()
         first_layer(0)
@@ -213,4 +211,4 @@ def tile_list_htabg_glu_noneP_kernel(
             second_layer(c - 2)
         for q in range(4):
             queue = nc.sync if q % 2 == 0 else nc.scalar
-            queue.dma_start(out_2[0, 4 * q : 4 * q + 4, :].bitcast(I32), y_sc[32 * q : 32 * q + 4, :].bitcast(I32))
+            queue.dma_start(out_2[0, q:16:4, :].bitcast(I32), y_sc[q:P:32, :].bitcast(I32))

@@ -20,7 +20,7 @@ P = 128
 PACK = 4
 GW = 256
 CW = 128
-VECTOR_CASTS_FROM = 4
+VECTOR_CASTS_FROM = 0
 
 
 def tile_list_htabg_glu_noneP_kernel(
@@ -141,7 +141,7 @@ def tile_list_htabg_glu_noneP_kernel(
 
         def first_layer(c):
             g, cols = divmod(c * CW, GW)[0], slice(c * CW % GW, c * CW % GW + CW)
-            ya = psum.tile([P, PACK, CW], F32, name="ya", bufs=2)
+            ya = psum.tile([P, PACK, CW], F32, name="ya", bufs=3)
             yb = psum.tile([P, PACK, CW], F32, name="yb", bufs=3)
             product(ya, 0, x_codes[g][:, cols], x_sc[g][:, cols])
             product(yb, 1, v_codes[:, c * CW : (c + 1) * CW], v_sc[:, c * CW : (c + 1) * CW])
@@ -161,7 +161,7 @@ def tile_list_htabg_glu_noneP_kernel(
 
         def second_layer(c):
             g, cols = divmod(c * CW, GW)[0], slice(c * CW % GW, c * CW % GW + CW)
-            y = psum.tile([P, PACK, CW], F32, name="y", bufs=3)
+            y = psum.tile([P, PACK, CW], F32, name="y", bufs=2)
             for u in range(PACK):
                 nc.tensor.matmul_mx(
                     y[:, u, :],
@@ -201,11 +201,11 @@ def tile_list_htabg_glu_noneP_kernel(
         prepare(0)
         prepare(1)
         quantise_wd()
+        prepare(2)
         first_layer(0)
         first_layer(1)
+        prepare(3)
         for c in range(2, chunks + 2):
-            if c % 2 == 0 and c // 2 + 1 < groups:
-                prepare(c // 2 + 1)
             if c < chunks:
                 first_layer(c)
             second_layer(c - 2)

@@ -14,13 +14,15 @@ U8 = mybir.dt.uint8
 FP8X4 = mybir.dt.float8_e4m3fn_x4
 FP4X4 = mybir.dt.float4_e2m1fn_x4
 MULT = mybir.AluOpType.mult
+ADD = mybir.AluOpType.add
+IS_EQUAL = mybir.AluOpType.is_equal
 SILU = mybir.ActivationFunctionType.Silu
 
 P = 128
 PACK = 4
 GW = 256
 CW = 128
-VECTOR_CASTS_FROM = 0
+PROMPT_CHUNKS = 2
 
 
 def tile_list_htabg_glu_noneP_kernel(
@@ -40,6 +42,18 @@ def tile_list_htabg_glu_noneP_kernel(
         tab_sc = keep.tile([P, T], U8, name="tab_sc", align_bytes=64)
         w_sc_raw = keep.tile([P, 2 * R], U8, name="w_sc_raw", align_bytes=64)
         nc.gpsimd.memset(tab_sc[:].bitcast(I32), 0)
+        ident = keep.tile([P, P], F32, name="ident")
+        ones = keep.tile([P, P], F32, name="ones")
+        column = keep.tile([P, P], F32, name="column", align_bytes=64)
+        row = keep.tile([P, P], F32, name="row", align_bytes=64)
+        nc.vector.memset(ones[:], 1.0)
+        nc.vector.memset(ident[:], 0.0)
+        nc.vector.tensor_tensor_scan(column[:], ones[:], ones[:], 0.0, MULT, ADD)
+        nc.vector.transpose(row[:], column[:])
+        for q in range(4):
+            block = slice(32 * q, 32 * (q + 1))
+            nc.vector.tensor_tensor(ident[block, block], column[block, block], row[block, block], IS_EQUAL)
+
         nc.vector.memset(w_sc_raw[:].bitcast(I32), 0)
 
         warm_in = keep.tile([P, 1], F32, name="warm_in")
@@ -50,18 +64,18 @@ def tile_list_htabg_glu_noneP_kernel(
         nc.sync.dma_start(head_list[:], offs2)
         nc.sync.dma_start(tab_list[:], offs)
         wgt = keep.tile([P, J], F32, name="wgt")
-        nc.sync.dma_start(wgt[:], wgt2)
+        wgt_rows = keep.tile([P, P], F32, name="wgt_rows")
+        nc.sync.dma_start(
+            wgt_rows[:], wgt2.rearrange("(g s) j -> g (s j)", s=16)[:, 0 : 2 * J].rearrange("g (m c) -> m g c", c=P)
+        )
         x_rows = xT.rearrange("(p i) t -> p i t", i=PACK)
         x_planes = [keep.tile([P, T], F32, name="x_plane%d" % i) for i in range(PACK)]
         for q in range(4):
             nc.sync.dma_start(tab_sc[q:P:32, :].bitcast(I32), tab_scales[0, q:16:4, :].bitcast(I32))
-        nc.sync.dma_start(x_planes[0][:], x_rows[:, 0, :])
         tab_w = keep.tile([P, T], I32, name="tab_w")
+        nc.sync.dma_start(tab_w[:], tab_words[0].rearrange("p t i -> p (t i)").bitcast(I32))
         for a, scales in enumerate((wa_scales, wb_scales)):
-            if a == 0:
-                nc.sync.dma_start(x_planes[1][:], x_rows[:, 1, :])
-            else:
-                nc.sync.dma_start(tab_w[:], tab_words[0].rearrange("p t i -> p (t i)").bitcast(I32))
+            nc.sync.dma_start(x_planes[a][:], x_rows[:, a, :])
             for q in range(4):
                 nc.sync.dma_start(
                     w_sc_raw[q:P:32, a * R : (a + 1) * R].bitcast(I32),
@@ -76,6 +90,21 @@ def tile_list_htabg_glu_noneP_kernel(
         wd_rows = wd.rearrange("(b t i) n -> t b i n", t=PACK, i=8)
         for t in range(PACK):
             nc.sync.dma_start(wd_raw[:, t, :], wd_rows[t])
+
+        turned = psum.tile([P, PACK, CW], F32, name="ya", bufs=3)
+        nc.tensor.transpose(turned[:, 0, :], wgt_rows[:], ident[:])
+        for half in range(2):
+            spread = keep.tile([P, PACK, P], F32, name="spread%d" % half)
+            nc.scalar.copy(
+                spread[:].rearrange("c r (g s e) -> c r g s e", s=2, e=8),
+                turned[:, 0, :].rearrange("c (s r g) -> c r g s", s=2, g=8)[:, PACK * half : PACK * (half + 1)]
+                .unsqueeze(4)
+                .to_broadcast([P, PACK, 8, 2, 8]),
+            )
+            back = psum.tile([P, PACK, CW], F32, name="y", bufs=2)
+            for r in range(PACK):
+                nc.tensor.transpose(back[:, r, :], spread[:, r, :], ident[:])
+            nc.scalar.copy(wgt[:, half * J // 2 : (half + 1) * J // 2], back[:].rearrange("p r c -> p (r c)"))
 
         v_sc = keep.tile([P, J], U8, name="v_sc", align_bytes=64)
         nc.vector.tensor_copy(v_sc[:], tab_sc[:].indirect(tab_list[:]))
@@ -149,15 +178,18 @@ def tile_list_htabg_glu_noneP_kernel(
             nc.scalar.activation(gate[:], ya[:].rearrange("p t j -> p j t"), SILU)
             h_bf = ring.tile([P, CW, PACK], BF16, name="h_bf", align_bytes=64)
             nc.vector.tensor_tensor(h_bf[:], yb[:].rearrange("p t j -> p j t"), gate[:], MULT)
+            return h_bf
+
+        def quantise_h(c, h_bf):
             nc.vector.quantize_mx(h_codes[c][:].bitcast(FP8X4), h_sc[c][:], h_bf[:].rearrange("p j t -> p (j t)"))
 
-        def quantise_wd():
-            wd_bf = keep.tile([P, N * PACK], BF16, name="wd_bf", align_bytes=64)
+        wd_bf = keep.tile([P, N * PACK], BF16, name="wd_bf", align_bytes=64)
+
+        def round_wd():
             nc.vector.tensor_copy(
                 wd_bf[:].rearrange("p (u m t) -> p m u t", u=PACK, t=PACK),
                 wd_raw[:].rearrange("p t (m u) -> p m u t", u=PACK),
             )
-            nc.vector.quantize_mx(wd_codes[:].bitcast(FP8X4), wd_sc[:], wd_bf[:])
 
         def second_layer(c):
             g, cols = divmod(c * CW, GW)[0], slice(c * CW % GW, c * CW % GW + CW)
@@ -175,40 +207,47 @@ def tile_list_htabg_glu_noneP_kernel(
             last = g == groups - 1
             staged = y_last[c % 2][:] if last else y_f32[g][:, :, cols]
             nc.scalar.copy(staged, y[:])
-            if c < VECTOR_CASTS_FROM:
-                nc.scalar.copy(y_bf[g][:, cols, :], y[:].rearrange("p t j -> p j t"))
-            if last:
-                hand_out(g, cols, staged)
-            elif c % 2 == 1:
-                hand_out(g, slice(0, GW), y_f32[g][:])
+            if not last and c % 2 == 0:
+                return []
+            if not last:
+                cols, staged = slice(0, GW), y_f32[g][:]
+            nc.sync.dma_start(out_rows[:, :, g * GW + cols.start : g * GW + cols.stop], staged)
+            nc.vector.tensor_copy(
+                y_bf[g][:, cols, :].rearrange("p (c i) t -> p c t i", i=4),
+                staged.rearrange("p t (c i) -> p c t i", i=4),
+            )
+            return [(g, cols)]
 
-        def hand_out(g, cols, staged):
+        def quantise_y(g, cols):
             places = slice(g * GW + cols.start, g * GW + cols.stop)
-            nc.sync.dma_start(out_rows[:, :, places], staged)
-            rounded = y_bf[g][:, cols, :].rearrange("p j t -> p (j t)")
-            if places.start >= VECTOR_CASTS_FROM * CW:
-                nc.vector.tensor_copy(
-                    rounded.rearrange("p (c i t) -> p c t i", i=4, t=PACK),
-                    staged.rearrange("p t (c i) -> p c t i", i=4),
-                )
-            nc.vector.quantize_mx(y_codes[g][:, cols].bitcast(FP8X4), y_sc[:, places], rounded)
+            nc.vector.quantize_mx(
+                y_codes[g][:, cols].bitcast(FP8X4), y_sc[:, places], y_bf[g][:, cols, :].rearrange("p j t -> p (j t)")
+            )
             if cols.stop == GW:
-                nc.scalar.dma_start(out_words[:, g * GW : (g + 1) * GW], y_codes[g][:]) if g == groups - 1 else nc.sync.dma_start(
-                    out_words[:, g * GW : (g + 1) * GW], y_codes[g][:]
-                )
+                queue = nc.scalar if g == groups - 1 else nc.sync
+                queue.dma_start(out_words[:, g * GW : (g + 1) * GW], y_codes[g][:])
 
         deal_words()
         prepare(0)
         prepare(1)
-        quantise_wd()
+        round_wd()
         prepare(2)
-        first_layer(0)
-        first_layer(1)
-        prepare(3)
-        for c in range(2, chunks + 2):
+        nc.vector.quantize_mx(wd_codes[:].bitcast(FP8X4), wd_sc[:], wd_bf[:])
+        deferred = range(PROMPT_CHUNKS, chunks - PROMPT_CHUNKS)
+        h_rounded = []
+        y_rounded = []
+        for c in range(chunks + 3):
             if c < chunks:
-                first_layer(c)
-            second_layer(c - 2)
+                h_rounded.append(first_layer(c))
+            if c < chunks and c not in deferred:
+                quantise_h(c, h_rounded[c])
+            if c == 1:
+                prepare(3)
+            for piece in y_rounded:
+                quantise_y(*piece)
+            if c - 1 in deferred:
+                quantise_h(c - 1, h_rounded[c - 1])
+            y_rounded = second_layer(c - 2) if 2 <= c < chunks + 2 else []
         for q in range(4):
             queue = nc.sync if q % 2 == 0 else nc.scalar
             queue.dma_start(out_2[0, q:16:4, :].bitcast(I32), y_sc[q:P:32, :].bitcast(I32))

@@ -22,7 +22,7 @@ P = 128
 PACK = 4
 GW = 256
 CW = 128
-PROMPT_CHUNKS = 2
+SCALAR_CHUNKS = (5, 6)
 
 
 def tile_list_htabg_glu_noneP_kernel(
@@ -41,7 +41,8 @@ def tile_list_htabg_glu_noneP_kernel(
         tab_list = keep.tile([P, J // 16], U16, name="tab_list")
         tab_sc = keep.tile([P, T], U8, name="tab_sc", align_bytes=64)
         w_sc_raw = keep.tile([P, 2 * R], U8, name="w_sc_raw", align_bytes=64)
-        nc.gpsimd.memset(tab_sc[:].bitcast(I32), 0)
+        nc.gpsimd.memset(tab_sc[:, : T // 2].bitcast(I32), 0)
+        nc.vector.memset(tab_sc[:, T // 2 :].bitcast(I32), 0)
         ident = keep.tile([P, P], F32, name="ident")
         ones = keep.tile([P, P], F32, name="ones")
         column = keep.tile([P, P], F32, name="column", align_bytes=64)
@@ -91,7 +92,7 @@ def tile_list_htabg_glu_noneP_kernel(
         for t in range(PACK):
             nc.sync.dma_start(wd_raw[:, t, :], wd_rows[t])
 
-        turned = psum.tile([P, PACK, CW], F32, name="ya", bufs=3)
+        turned = psum.tile([P, PACK, CW], F32, name="turned", tag="ya_y", bufs=5)
         nc.tensor.transpose(turned[:, 0, :], wgt_rows[:], ident[:])
         for half in range(2):
             spread = keep.tile([P, PACK, P], F32, name="spread%d" % half)
@@ -101,7 +102,7 @@ def tile_list_htabg_glu_noneP_kernel(
                 .unsqueeze(4)
                 .to_broadcast([P, PACK, 8, 2, 8]),
             )
-            back = psum.tile([P, PACK, CW], F32, name="y", bufs=2)
+            back = psum.tile([P, PACK, CW], F32, name="back", tag="ya_y", bufs=5)
             for r in range(PACK):
                 nc.tensor.transpose(back[:, r, :], spread[:, r, :], ident[:])
             nc.scalar.copy(wgt[:, half * J // 2 : (half + 1) * J // 2], back[:].rearrange("p r c -> p (r c)"))
@@ -138,10 +139,9 @@ def tile_list_htabg_glu_noneP_kernel(
         x_sc = [keep.tile([P, GW], U8, name="x_sc%d" % g, align_bytes=64) for g in range(groups)]
         wd_codes = keep.tile([P, N], U32, name="wd_codes", align_bytes=64)
         wd_sc = keep.tile([P, N], U8, name="wd_sc", align_bytes=64)
-        y_codes = [keep.tile([P, GW], I32, name="y_codes%d" % g, align_bytes=64) for g in range(groups)]
+        y_codes = keep.tile([P, J], I32, name="y_codes", align_bytes=64)
         y_sc = keep.tile([P, J], U8, name="y_sc", align_bytes=64)
-        y_f32 = [keep.tile([P, PACK, GW], F32, name="y_f32_%d" % g) for g in range(groups - 1)]
-        y_last = [keep.tile([P, PACK, CW], F32, name="y_last%d" % e) for e in range(2)]
+        y_f32 = [keep.tile([P, PACK, GW], F32, name="y_f32_%d" % g) for g in range(groups)]
         y_bf = [keep.tile([P, GW, PACK], BF16, name="y_bf%d" % g, align_bytes=64) for g in range(groups)]
         h_codes = [keep.tile([P, CW], U32, name="h_codes%d" % c, align_bytes=64) for c in range(chunks)]
         h_sc = [keep.tile([P, CW], U8, name="h_sc%d" % c, align_bytes=64) for c in range(chunks)]
@@ -155,6 +155,8 @@ def tile_list_htabg_glu_noneP_kernel(
             )
             nc.scalar.copy(x_bf[g][:, :, 2:4], picked_hi[:, :, cols].rearrange("p t j -> p j t"))
             nc.vector.quantize_mx(x_codes[g][:].bitcast(FP8X4), x_sc[g][:], x_bf[g][:].rearrange("p j t -> p (j t)"))
+            gate(2 * g)
+            gate(2 * g + 1)
 
         def product(bank, a, codes, scales):
             for t in range(PACK):
@@ -168,16 +170,19 @@ def tile_list_htabg_glu_noneP_kernel(
                     stop=True,
                 )
 
-        def first_layer(c):
+        gates = [keep.tile([P, CW, PACK], F32, name="gate%d" % c) for c in range(chunks)]
+
+        def gate(c):
             g, cols = divmod(c * CW, GW)[0], slice(c * CW % GW, c * CW % GW + CW)
-            ya = psum.tile([P, PACK, CW], F32, name="ya", bufs=3)
-            yb = psum.tile([P, PACK, CW], F32, name="yb", bufs=3)
+            ya = psum.tile([P, PACK, CW], F32, name="ya", tag="ya_y", bufs=5)
             product(ya, 0, x_codes[g][:, cols], x_sc[g][:, cols])
+            nc.scalar.activation(gates[c][:], ya[:].rearrange("p t j -> p j t"), SILU)
+
+        def first_layer(c):
+            yb = psum.tile([P, PACK, CW], F32, name="yb", bufs=3)
             product(yb, 1, v_codes[:, c * CW : (c + 1) * CW], v_sc[:, c * CW : (c + 1) * CW])
-            gate = ring.tile([P, CW, PACK], F32, name="gate", bufs=chunks)
-            nc.scalar.activation(gate[:], ya[:].rearrange("p t j -> p j t"), SILU)
             h_bf = ring.tile([P, CW, PACK], BF16, name="h_bf", align_bytes=64)
-            nc.vector.tensor_tensor(h_bf[:], yb[:].rearrange("p t j -> p j t"), gate[:], MULT)
+            nc.vector.tensor_tensor(h_bf[:], yb[:].rearrange("p t j -> p j t"), gates[c][:], MULT)
             return h_bf
 
         def quantise_h(c, h_bf):
@@ -191,9 +196,11 @@ def tile_list_htabg_glu_noneP_kernel(
                 wd_raw[:].rearrange("p t (m u) -> p m u t", u=PACK),
             )
 
+        y_banks = []
+
         def second_layer(c):
             g, cols = divmod(c * CW, GW)[0], slice(c * CW % GW, c * CW % GW + CW)
-            y = psum.tile([P, PACK, CW], F32, name="y", bufs=2)
+            y = psum.tile([P, PACK, CW], F32, name="y", tag="ya_y", bufs=5)
             for u in range(PACK):
                 nc.tensor.matmul_mx(
                     y[:, u, :],
@@ -204,50 +211,65 @@ def tile_list_htabg_glu_noneP_kernel(
                     start=True,
                     stop=True,
                 )
-            last = g == groups - 1
-            staged = y_last[c % 2][:] if last else y_f32[g][:, :, cols]
-            nc.scalar.copy(staged, y[:])
-            if not last and c % 2 == 0:
-                return []
-            if not last:
-                cols, staged = slice(0, GW), y_f32[g][:]
-            nc.sync.dma_start(out_rows[:, :, g * GW + cols.start : g * GW + cols.stop], staged)
+            nc.scalar.copy(y_f32[g][:, :, cols], y[:])
+            y_banks.append((y_bf[g][:, cols, :], y))
+            if c - 1 in SCALAR_CHUNKS:
+                rounded, bank = y_banks[c - 1]
+                nc.scalar.copy(rounded, bank[:].rearrange("p t j -> p j t"))
+            if g == groups - 1:
+                nc.sync.dma_start(out_rows[:, :, c * CW : (c + 1) * CW], y_f32[g][:, :, cols])
+            elif c % 2 == 1:
+                nc.sync.dma_start(out_rows[:, :, g * GW : (g + 1) * GW], y_f32[g][:])
+
+        def round_y(g, cols):
             nc.vector.tensor_copy(
                 y_bf[g][:, cols, :].rearrange("p (c i) t -> p c t i", i=4),
-                staged.rearrange("p t (c i) -> p c t i", i=4),
+                y_f32[g][:, :, cols].rearrange("p t (c i) -> p c t i", i=4),
             )
-            return [(g, cols)]
 
         def quantise_y(g, cols):
-            places = slice(g * GW + cols.start, g * GW + cols.stop)
             nc.vector.quantize_mx(
-                y_codes[g][:, cols].bitcast(FP8X4), y_sc[:, places], y_bf[g][:, cols, :].rearrange("p j t -> p (j t)")
+                y_codes[:, g * GW + cols.start : g * GW + cols.stop].bitcast(FP8X4),
+                y_sc[:, g * GW + cols.start : g * GW + cols.stop],
+                y_bf[g][:, cols, :].rearrange("p j t -> p (j t)"),
             )
-            if cols.stop == GW:
-                queue = nc.scalar if g == groups - 1 else nc.sync
-                queue.dma_start(out_words[:, g * GW : (g + 1) * GW], y_codes[g][:])
+
+        def store_words(queue, first, stop):
+            queue.dma_start(out_words[:, first:stop], y_codes[:, first:stop])
 
         deal_words()
         prepare(0)
         prepare(1)
-        round_wd()
         prepare(2)
+        round_wd()
+        prepare(3)
+        h_rounded = [first_layer(0)]
         nc.vector.quantize_mx(wd_codes[:].bitcast(FP8X4), wd_sc[:], wd_bf[:])
-        deferred = range(PROMPT_CHUNKS, chunks - PROMPT_CHUNKS)
-        h_rounded = []
-        y_rounded = []
-        for c in range(chunks + 3):
-            if c < chunks:
-                h_rounded.append(first_layer(c))
-            if c < chunks and c not in deferred:
-                quantise_h(c, h_rounded[c])
-            if c == 1:
-                prepare(3)
-            for piece in y_rounded:
-                quantise_y(*piece)
-            if c - 1 in deferred:
-                quantise_h(c - 1, h_rounded[c - 1])
-            y_rounded = second_layer(c - 2) if 2 <= c < chunks + 2 else []
+        whole, front, back_half = slice(0, GW), slice(0, CW), slice(CW, GW)
+        quantise_h(0, h_rounded[0])
+        second_layer(0)
+        h_rounded.append(first_layer(1))
+        for c in range(1, chunks):
+            if c + 1 < chunks - 1:
+                h_rounded.append(first_layer(c + 1))
+            quantise_h(c, h_rounded[c])
+            second_layer(c)
+            if c == 3:
+                round_y(0, whole)
+            if c == 4:
+                quantise_y(0, whole)
+                store_words(nc.sync, 0, GW)
+            if c + 1 == chunks - 1:
+                h_rounded.append(first_layer(c + 1))
+        round_y(1, whole)
+        round_y(2, front)
+        quantise_y(1, whole)
+        store_words(nc.sync, GW, 2 * GW)
+        round_y(3, back_half)
+        quantise_y(2, whole)
+        store_words(nc.sync, 2 * GW, 3 * GW)
+        quantise_y(3, whole)
+        store_words(nc.scalar, 3 * GW, J)
         for q in range(4):
             queue = nc.sync if q % 2 == 0 else nc.scalar
             queue.dma_start(out_2[0, q:16:4, :].bitcast(I32), y_sc[q:P:32, :].bitcast(I32))

@@ -213,9 +213,6 @@ def tile_list_htabg_glu_noneP_kernel(
                 )
             nc.scalar.copy(y_f32[g][:, :, cols], y[:])
             y_banks.append((y_bf[g][:, cols, :], y))
-            if c - 1 in SCALAR_CHUNKS:
-                rounded, bank = y_banks[c - 1]
-                nc.scalar.copy(rounded, bank[:].rearrange("p t j -> p j t"))
             if g == groups - 1:
                 nc.sync.dma_start(out_rows[:, :, c * CW : (c + 1) * CW], y_f32[g][:, :, cols])
             elif c % 2 == 1:
@@ -254,22 +251,21 @@ def tile_list_htabg_glu_noneP_kernel(
                 h_rounded.append(first_layer(c + 1))
             quantise_h(c, h_rounded[c])
             second_layer(c)
-            if c == 3:
-                round_y(0, whole)
-            if c == 4:
-                quantise_y(0, whole)
-                store_words(nc.sync, 0, GW)
             if c + 1 == chunks - 1:
                 h_rounded.append(first_layer(c + 1))
+        for c in SCALAR_CHUNKS:
+            rounded, bank = y_banks[c]
+            nc.scalar.copy(rounded, bank[:].rearrange("p t j -> p j t"))
+        round_y(0, whole)
         round_y(1, whole)
+        quantise_y(0, whole)
         round_y(2, front)
         quantise_y(1, whole)
-        store_words(nc.sync, GW, 2 * GW)
+        store_words(nc.sync, 0, 2 * GW)
         round_y(3, back_half)
         quantise_y(2, whole)
-        store_words(nc.sync, 2 * GW, 3 * GW)
         quantise_y(3, whole)
-        store_words(nc.scalar, 3 * GW, J)
+        store_words(nc.scalar, 2 * GW, J)
         for q in range(4):
             queue = nc.sync if q % 2 == 0 else nc.scalar
             queue.dma_start(out_2[0, q:16:4, :].bitcast(I32), y_sc[q:P:32, :].bitcast(I32))

@@ -48,7 +48,7 @@ def tile_list_htabg_glu_noneP_kernel(
         column = keep.tile([P, P], F32, name="column", align_bytes=64)
         row = keep.tile([P, P], F32, name="row", align_bytes=64)
         nc.vector.memset(ones[:], 1.0)
-        nc.vector.memset(ident[:], 0.0)
+        nc.scalar.activation(ident[:], ones[:], SILU, scale=0.0)
         nc.vector.tensor_tensor_scan(column[:], ones[:], ones[:], 0.0, MULT, ADD)
         nc.vector.transpose(row[:], column[:])
         for q in range(4):
@@ -56,11 +56,8 @@ def tile_list_htabg_glu_noneP_kernel(
             nc.vector.tensor_tensor(ident[block, block], column[block, block], row[block, block], IS_EQUAL)
 
         nc.vector.memset(w_sc_raw[:].bitcast(I32), 0)
-
-        warm_in = keep.tile([P, 1], F32, name="warm_in")
-        warm_out = keep.tile([P, 1], F32, name="warm_out")
-        nc.vector.memset(warm_in[:], 0.0)
-        nc.scalar.activation(warm_out[:], warm_in[:], SILU)
+        v_sc = keep.tile([P, J], U8, name="v_sc", align_bytes=64)
+        nc.vector.memset(v_sc[:].bitcast(I32), 0)
 
         nc.sync.dma_start(head_list[:], offs2)
         nc.sync.dma_start(tab_list[:], offs)
@@ -71,8 +68,9 @@ def tile_list_htabg_glu_noneP_kernel(
         )
         x_rows = xT.rearrange("(p i) t -> p i t", i=PACK)
         x_planes = [keep.tile([P, T], F32, name="x_plane%d" % i) for i in range(PACK)]
-        for q in range(4):
-            nc.sync.dma_start(tab_sc[q:P:32, :].bitcast(I32), tab_scales[0, q:16:4, :].bitcast(I32))
+        nc.sync.dma_start(tab_sc[0:P:8, :].bitcast(I32), tab_scales[0].bitcast(I32))
+        v_sc_spaced = keep.tile([P, J], U8, name="v_sc_spaced", align_bytes=64)
+        nc.vector.tensor_copy(v_sc_spaced[:], tab_sc[:].indirect(tab_list[:]))
         tab_w = keep.tile([P, T], I32, name="tab_w")
         nc.sync.dma_start(tab_w[:], tab_words[0].rearrange("p t i -> p (t i)").bitcast(I32))
         for a, scales in enumerate((wa_scales, wb_scales)):
@@ -86,6 +84,8 @@ def tile_list_htabg_glu_noneP_kernel(
         for a, words in enumerate((wa_words, wb_words)):
             nc.sync.dma_start(w_raw[:, a, :].bitcast(I32), words[0].bitcast(I32))
         nc.sync.dma_start(x_planes[2][:], x_rows[:, 2, :])
+        for q in range(4):
+            nc.sync.dma_start(v_sc[q:P:32, :].bitcast(I32), v_sc_spaced[8 * q : P : 32, :].bitcast(I32))
         nc.sync.dma_start(x_planes[3][:], x_rows[:, 3, :])
         wd_raw = keep.tile([P, PACK, N], F32, name="wd_raw")
         wd_rows = wd.rearrange("(b t i) n -> t b i n", t=PACK, i=8)
@@ -106,9 +106,6 @@ def tile_list_htabg_glu_noneP_kernel(
             for r in range(PACK):
                 nc.tensor.transpose(back[:, r, :], spread[:, r, :], ident[:])
             nc.scalar.copy(wgt[:, half * J // 2 : (half + 1) * J // 2], back[:].rearrange("p r c -> p (r c)"))
-
-        v_sc = keep.tile([P, J], U8, name="v_sc", align_bytes=64)
-        nc.vector.tensor_copy(v_sc[:], tab_sc[:].indirect(tab_list[:]))
 
         x_bf = [keep.tile([P, GW, PACK], BF16, name="x_bf%d" % g, align_bytes=64) for g in range(groups)]
         picked_lo = keep.tile([P, 2, J], F32, name="picked_lo")

@@ -22,6 +22,7 @@ P = 128
 PACK = 4
 GW = 256
 CW = 128
+SPARE = P - 16
 SCALAR_CHUNKS = (5, 6)
 
 
@@ -41,14 +42,15 @@ def tile_list_htabg_glu_noneP_kernel(
         tab_list = keep.tile([P, J // 16], U16, name="tab_list")
         tab_sc = keep.tile([P, T], U8, name="tab_sc", align_bytes=64)
         w_sc_raw = keep.tile([P, 2 * R], U8, name="w_sc_raw", align_bytes=64)
-        nc.gpsimd.memset(tab_sc[:, : T // 2].bitcast(I32), 0)
-        nc.vector.memset(tab_sc[:, T // 2 :].bitcast(I32), 0)
+        nc.gpsimd.memset(tab_sc[0:SPARE, :].bitcast(I32), 0)
         ident = keep.tile([P, P], F32, name="ident")
         ones = keep.tile([P, P], F32, name="ones")
         column = keep.tile([P, P], F32, name="column", align_bytes=64)
         row = keep.tile([P, P], F32, name="row", align_bytes=64)
         nc.vector.memset(ones[:], 1.0)
-        nc.scalar.activation(ident[:], ones[:], SILU, scale=0.0)
+        nc.scalar.activation(ident[0:32, 32:P], ones[0:32, 32:P], SILU, scale=0.0)
+        nc.vector.memset(ident[32:64, :], 0.0)
+        nc.vector.memset(ident[64:P, :], 0.0)
         nc.vector.tensor_tensor_scan(column[:], ones[:], ones[:], 0.0, MULT, ADD)
         nc.vector.transpose(row[:], column[:])
         for q in range(4):
@@ -59,33 +61,38 @@ def tile_list_htabg_glu_noneP_kernel(
         v_sc = keep.tile([P, J], U8, name="v_sc", align_bytes=64)
         nc.vector.memset(v_sc[:].bitcast(I32), 0)
 
-        nc.sync.dma_start(head_list[:], offs2)
         nc.sync.dma_start(tab_list[:], offs)
+        nc.sync.dma_start(tab_sc[SPARE:P, :].bitcast(I32), tab_scales[0].bitcast(I32))
         wgt = keep.tile([P, J], F32, name="wgt")
         wgt_rows = keep.tile([P, P], F32, name="wgt_rows")
-        nc.sync.dma_start(
+        nc.scalar.dma_start(
             wgt_rows[:], wgt2.rearrange("(g s) j -> g (s j)", s=16)[:, 0 : 2 * J].rearrange("g (m c) -> m g c", c=P)
         )
         x_rows = xT.rearrange("(p i) t -> p i t", i=PACK)
         x_planes = [keep.tile([P, T], F32, name="x_plane%d" % i) for i in range(PACK)]
-        nc.sync.dma_start(tab_sc[0:P:8, :].bitcast(I32), tab_scales[0].bitcast(I32))
         v_sc_spaced = keep.tile([P, J], U8, name="v_sc_spaced", align_bytes=64)
         nc.vector.tensor_copy(v_sc_spaced[:], tab_sc[:].indirect(tab_list[:]))
         tab_w = keep.tile([P, T], I32, name="tab_w")
         nc.sync.dma_start(tab_w[:], tab_words[0].rearrange("p t i -> p (t i)").bitcast(I32))
-        for a, scales in enumerate((wa_scales, wb_scales)):
-            nc.sync.dma_start(x_planes[a][:], x_rows[:, a, :])
+        nc.sync.dma_start(head_list[:], offs2)
+        w_raw = [keep.tile([P, 2 * R], U8, name="w_raw%d" % a) for a in range(2)]
+
+        def load_scales(a, scales):
             for q in range(4):
                 nc.sync.dma_start(
                     w_sc_raw[q:P:32, a * R : (a + 1) * R].bitcast(I32),
                     scales[0, q:16:4, :].bitcast(I32),
                 )
-        w_raw = keep.tile([P, 2, 2 * R], U8, name="w_raw")
-        for a, words in enumerate((wa_words, wb_words)):
-            nc.sync.dma_start(w_raw[:, a, :].bitcast(I32), words[0].bitcast(I32))
+
+        nc.sync.dma_start(x_planes[0][:], x_rows[:, 0, :])
+        load_scales(0, wa_scales)
+        nc.sync.dma_start(w_raw[0][:].bitcast(I32), wa_words[0].bitcast(I32))
+        nc.sync.dma_start(x_planes[1][:], x_rows[:, 1, :])
+        nc.sync.dma_start(w_raw[1][:].bitcast(I32), wb_words[0].bitcast(I32))
+        load_scales(1, wb_scales)
         nc.sync.dma_start(x_planes[2][:], x_rows[:, 2, :])
         for q in range(4):
-            nc.sync.dma_start(v_sc[q:P:32, :].bitcast(I32), v_sc_spaced[8 * q : P : 32, :].bitcast(I32))
+            nc.sync.dma_start(v_sc[q:P:32, :].bitcast(I32), v_sc_spaced[SPARE + q : P : 4, :].bitcast(I32))
         nc.sync.dma_start(x_planes[3][:], x_rows[:, 3, :])
         wd_raw = keep.tile([P, PACK, N], F32, name="wd_raw")
         wd_rows = wd.rearrange("(b t i) n -> t b i n", t=PACK, i=8)
@@ -95,7 +102,7 @@ def tile_list_htabg_glu_noneP_kernel(
         turned = psum.tile([P, PACK, CW], F32, name="turned", tag="ya_y", bufs=5)
         nc.tensor.transpose(turned[:, 0, :], wgt_rows[:], ident[:])
         for half in range(2):
-            spread = keep.tile([P, PACK, P], F32, name="spread%d" % half)
+            spread = keep.tile([P, PACK, P], F32, name="spread%d" % half, align_bytes=64)
             nc.scalar.copy(
                 spread[:].rearrange("c r (g s e) -> c r g s e", s=2, e=8),
                 turned[:, 0, :].rearrange("c (s r g) -> c r g s", s=2, g=8)[:, PACK * half : PACK * (half + 1)]
@@ -107,11 +114,19 @@ def tile_list_htabg_glu_noneP_kernel(
                 nc.tensor.transpose(back[:, r, :], spread[:, r, :], ident[:])
             nc.scalar.copy(wgt[:, half * J // 2 : (half + 1) * J // 2], back[:].rearrange("p r c -> p (r c)"))
 
-        x_bf = [keep.tile([P, GW, PACK], BF16, name="x_bf%d" % g, align_bytes=64) for g in range(groups)]
+        x_pairs = [keep.tile([P, 2 * GW * PACK], BF16, name="x_pair%d" % g, align_bytes=64) for g in range(groups // 2)]
+        x_bf = [
+            x_pairs[g // 2][:, g % 2 * GW * PACK : (g % 2 + 1) * GW * PACK].rearrange("p (j t) -> p j t", t=PACK)
+            for g in range(groups)
+        ]
         picked_lo = keep.tile([P, 2, J], F32, name="picked_lo")
-        picked_hi = keep.tile([P, 2, J], F32, name="picked_hi")
+        picked_hi = keep.tile([P, 2, J], F32, name="picked_hi", align_bytes=64)
         for i in range(2):
-            nc.vector.tensor_tensor(picked_lo[:, i, :], x_planes[i][:].indirect(head_list[:]), wgt[:], MULT)
+            for half in range(2):
+                cols = slice(half * J // 2, (half + 1) * J // 2)
+                nc.vector.tensor_tensor(
+                    picked_lo[:, i, cols], x_planes[i][:].indirect(head_list[:, cols.start // 16 : cols.stop // 16]), wgt[:, cols], MULT
+                )
         for g in range(groups):
             nc.scalar.copy(x_bf[g][:, :, 0:2], picked_lo[:, :, g * GW : (g + 1) * GW].rearrange("p t j -> p j t"))
         v_codes = keep.tile([P, J], U32, name="v_codes", align_bytes=64)
@@ -119,17 +134,17 @@ def tile_list_htabg_glu_noneP_kernel(
 
         nc.vector.tensor_tensor(picked_hi[:, 0, :], x_planes[2][:].indirect(head_list[:]), wgt[:], MULT)
 
-        w_sc = keep.tile([P, 2 * R], U8, name="w_sc", align_bytes=64)
-        nc.vector.tensor_copy(
-            w_sc[:].bitcast(I32).rearrange("p (a t b w) -> p a t b w", a=2, t=PACK, w=2),
-            w_sc_raw[:].bitcast(I32).rearrange("p (a b t w) -> p a t b w", a=2, t=PACK, w=2),
-        )
-        w_codes = keep.tile([P, 2, 2 * R], U8, name="w_codes", align_bytes=64)
-
-        def deal_words():
-            nc.vector.tensor_copy(
-                w_codes[:].bitcast(I32).rearrange("p a (t b w) -> p a t b w", t=PACK, w=4),
-                w_raw[:].bitcast(I32).rearrange("p a (b t w) -> p a t b w", t=PACK, w=4),
+        dealt = keep.tile([P, 6 * R], U8, name="dealt", tag="spread1", align_bytes=64)
+        w_sc = dealt[:, 4 * R :]
+        w_codes = dealt[:, : 4 * R].rearrange("p (a c) -> p a c", a=2)
+        for a in range(2):
+            nc.scalar.copy(
+                w_sc[:, a * R : (a + 1) * R].bitcast(U32).rearrange("p (t b w) -> p t b w", t=PACK, w=2),
+                w_sc_raw[:, a * R : (a + 1) * R].bitcast(U32).rearrange("p (b t w) -> p t b w", t=PACK, w=2),
+            )
+            nc.scalar.copy(
+                w_codes[:, a, :].bitcast(U32).rearrange("p (t b w) -> p t b w", t=PACK, w=4),
+                w_raw[a][:].bitcast(U32).rearrange("p (b t w) -> p t b w", t=PACK, w=4),
             )
 
         x_codes = [keep.tile([P, GW], U32, name="x_codes%d" % g, align_bytes=64) for g in range(groups)]
@@ -151,9 +166,7 @@ def tile_list_htabg_glu_noneP_kernel(
                 picked_hi[:, 1, cols], x_planes[3][:].indirect(head_list[:, g * GW // 16 : (g + 1) * GW // 16]), wgt[:, cols], MULT
             )
             nc.scalar.copy(x_bf[g][:, :, 2:4], picked_hi[:, :, cols].rearrange("p t j -> p j t"))
-            nc.vector.quantize_mx(x_codes[g][:].bitcast(FP8X4), x_sc[g][:], x_bf[g][:].rearrange("p j t -> p (j t)"))
-            gate(2 * g)
-            gate(2 * g + 1)
+            nc.vector.quantize_mx(x_codes[g][:].bitcast(FP8X4), x_sc[g][:], x_bf[g].rearrange("p j t -> p (j t)"))
 
         def product(bank, a, codes, scales):
             for t in range(PACK):
@@ -185,11 +198,11 @@ def tile_list_htabg_glu_noneP_kernel(
         def quantise_h(c, h_bf):
             nc.vector.quantize_mx(h_codes[c][:].bitcast(FP8X4), h_sc[c][:], h_bf[:].rearrange("p j t -> p (j t)"))
 
-        wd_bf = keep.tile([P, N * PACK], BF16, name="wd_bf", align_bytes=64)
+        wd_bf = x_pairs[0][:]
 
         def round_wd():
             nc.vector.tensor_copy(
-                wd_bf[:].rearrange("p (u m t) -> p m u t", u=PACK, t=PACK),
+                wd_bf.rearrange("p (u m t) -> p m u t", u=PACK, t=PACK),
                 wd_raw[:].rearrange("p t (m u) -> p m u t", u=PACK),
             )
 
@@ -231,14 +244,15 @@ def tile_list_htabg_glu_noneP_kernel(
         def store_words(queue, first, stop):
             queue.dma_start(out_words[:, first:stop], y_codes[:, first:stop])
 
-        deal_words()
         prepare(0)
         prepare(1)
         prepare(2)
-        round_wd()
         prepare(3)
+        round_wd()
+        for c in range(chunks):
+            gate(c)
         h_rounded = [first_layer(0)]
-        nc.vector.quantize_mx(wd_codes[:].bitcast(FP8X4), wd_sc[:], wd_bf[:])
+        nc.vector.quantize_mx(wd_codes[:].bitcast(FP8X4), wd_sc[:], wd_bf)
         whole, front, back_half = slice(0, GW), slice(0, CW), slice(CW, GW)
         quantise_h(0, h_rounded[0])
         second_layer(0)

@@ -223,9 +223,7 @@ def tile_list_htabg_glu_noneP_kernel(
                 )
             nc.scalar.copy(y_f32[g][:, :, cols], y[:])
             y_banks.append((y_bf[g][:, cols, :], y))
-            if g == groups - 1:
-                nc.sync.dma_start(out_rows[:, :, c * CW : (c + 1) * CW], y_f32[g][:, :, cols])
-            elif c % 2 == 1:
+            if c % 2 == 1:
                 nc.sync.dma_start(out_rows[:, :, g * GW : (g + 1) * GW], y_f32[g][:])
 
         def round_y(g, cols):

@@ -23,7 +23,7 @@ PACK = 4
 GW = 256
 CW = 128
 SPARE = P - 16
-SCALAR_CHUNKS = (5, 6)
+SCALAR_CHUNKS = (6,)
 
 
 def tile_list_htabg_glu_noneP_kernel(
@@ -121,12 +121,12 @@ def tile_list_htabg_glu_noneP_kernel(
         ]
         picked_lo = keep.tile([P, 2, J], F32, name="picked_lo")
         picked_hi = keep.tile([P, 2, J], F32, name="picked_hi", align_bytes=64)
-        for i in range(2):
-            for half in range(2):
-                cols = slice(half * J // 2, (half + 1) * J // 2)
-                nc.vector.tensor_tensor(
-                    picked_lo[:, i, cols], x_planes[i][:].indirect(head_list[:, cols.start // 16 : cols.stop // 16]), wgt[:, cols], MULT
-                )
+        nc.vector.tensor_tensor(picked_lo[:, 0, :], x_planes[0][:].indirect(head_list[:]), wgt[:], MULT)
+        for half in range(2):
+            cols = slice(half * J // 2, (half + 1) * J // 2)
+            nc.vector.tensor_tensor(
+                picked_lo[:, 1, cols], x_planes[1][:].indirect(head_list[:, cols.start // 16 : cols.stop // 16]), wgt[:, cols], MULT
+            )
         for g in range(groups):
             nc.scalar.copy(x_bf[g][:, :, 0:2], picked_lo[:, :, g * GW : (g + 1) * GW].rearrange("p t j -> p j t"))
         v_codes = keep.tile([P, J], U32, name="v_codes", align_bytes=64)
@@ -251,7 +251,7 @@ def tile_list_htabg_glu_noneP_kernel(
             gate(c)
         h_rounded = [first_layer(0)]
         nc.vector.quantize_mx(wd_codes[:].bitcast(FP8X4), wd_sc[:], wd_bf)
-        whole, front, back_half = slice(0, GW), slice(0, CW), slice(CW, GW)
+        whole, back_half = slice(0, GW), slice(CW, GW)
         quantise_h(0, h_rounded[0])
         second_layer(0)
         h_rounded.append(first_layer(1))
@@ -268,9 +268,9 @@ def tile_list_htabg_glu_noneP_kernel(
         round_y(0, whole)
         round_y(1, whole)
         quantise_y(0, whole)
-        round_y(2, front)
         quantise_y(1, whole)
         store_words(nc.sync, 0, 2 * GW)
+        round_y(2, whole)
         round_y(3, back_half)
         quantise_y(2, whole)
         quantise_y(3, whole)

@@ -23,7 +23,8 @@ PACK = 4
 GW = 256
 CW = 128
 SPARE = P - 16
-SCALAR_CHUNKS = (6,)
+WD_VECTOR = 32
+AHEAD = 4
 
 
 def tile_list_htabg_glu_noneP_kernel(
@@ -35,7 +36,6 @@ def tile_list_htabg_glu_noneP_kernel(
     chunks = J // CW
     with ExitStack() as ctx:
         keep = ctx.enter_context(tc.tile_pool(name="keep", bufs=1))
-        ring = ctx.enter_context(tc.tile_pool(name="ring", bufs=3))
         psum = ctx.enter_context(tc.psum_pool(name="psum", bufs=1))
 
         head_list = keep.tile([P, J // 16], U16, name="head_list")
@@ -94,7 +94,7 @@ def tile_list_htabg_glu_noneP_kernel(
         for q in range(4):
             nc.sync.dma_start(v_sc[q:P:32, :].bitcast(I32), v_sc_spaced[SPARE + q : P : 4, :].bitcast(I32))
         nc.sync.dma_start(x_planes[3][:], x_rows[:, 3, :])
-        wd_raw = keep.tile([P, PACK, N], F32, name="wd_raw")
+        wd_raw = keep.tile([P, PACK, N], F32, name="wd_raw", align_bytes=64)
         wd_rows = wd.rearrange("(b t i) n -> t b i n", t=PACK, i=8)
         for t in range(PACK):
             nc.sync.dma_start(wd_raw[:, t, :], wd_rows[t])
@@ -151,11 +151,8 @@ def tile_list_htabg_glu_noneP_kernel(
         x_sc = [keep.tile([P, GW], U8, name="x_sc%d" % g, align_bytes=64) for g in range(groups)]
         wd_codes = keep.tile([P, N], U32, name="wd_codes", align_bytes=64)
         wd_sc = keep.tile([P, N], U8, name="wd_sc", align_bytes=64)
-        y_codes = keep.tile([P, J], I32, name="y_codes", align_bytes=64)
         y_sc = keep.tile([P, J], U8, name="y_sc", align_bytes=64)
         y_f32 = [keep.tile([P, PACK, GW], F32, name="y_f32_%d" % g) for g in range(groups)]
-        y_bf = [keep.tile([P, GW, PACK], BF16, name="y_bf%d" % g, align_bytes=64) for g in range(groups)]
-        h_codes = [keep.tile([P, CW], U32, name="h_codes%d" % c, align_bytes=64) for c in range(chunks)]
         h_sc = [keep.tile([P, CW], U8, name="h_sc%d" % c, align_bytes=64) for c in range(chunks)]
         out_rows = out_0.rearrange("(p t) j -> p t j", t=PACK)
         out_words = out_1[0].rearrange("p j i -> p (j i)").bitcast(I32)
@@ -165,7 +162,10 @@ def tile_list_htabg_glu_noneP_kernel(
             nc.vector.tensor_tensor(
                 picked_hi[:, 1, cols], x_planes[3][:].indirect(head_list[:, g * GW // 16 : (g + 1) * GW // 16]), wgt[:, cols], MULT
             )
-            nc.scalar.copy(x_bf[g][:, :, 2:4], picked_hi[:, :, cols].rearrange("p t j -> p j t"))
+            if g < groups - 1:
+                nc.scalar.copy(x_bf[g][:, :, 2:4], picked_hi[:, :, cols].rearrange("p t j -> p j t"))
+
+        def quantise_x(g):
             nc.vector.quantize_mx(x_codes[g][:].bitcast(FP8X4), x_sc[g][:], x_bf[g].rearrange("p j t -> p (j t)"))
 
         def product(bank, a, codes, scales):
@@ -180,7 +180,7 @@ def tile_list_htabg_glu_noneP_kernel(
                     stop=True,
                 )
 
-        gates = [keep.tile([P, CW, PACK], F32, name="gate%d" % c) for c in range(chunks)]
+        gates = [keep.tile([P, CW, PACK], F32, name="gate%d" % c, align_bytes=64) for c in range(chunks)]
 
         def gate(c):
             g, cols = divmod(c * CW, GW)[0], slice(c * CW % GW, c * CW % GW + CW)
@@ -191,22 +191,14 @@ def tile_list_htabg_glu_noneP_kernel(
         def first_layer(c):
             yb = psum.tile([P, PACK, CW], F32, name="yb", bufs=3)
             product(yb, 1, v_codes[:, c * CW : (c + 1) * CW], v_sc[:, c * CW : (c + 1) * CW])
-            h_bf = ring.tile([P, CW, PACK], BF16, name="h_bf", align_bytes=64)
-            nc.vector.tensor_tensor(h_bf[:], yb[:].rearrange("p t j -> p j t"), gates[c][:], MULT)
-            return h_bf
+            nc.vector.tensor_tensor(h_bf[c], yb[:].rearrange("p t j -> p j t"), gates[c][:], MULT)
 
-        def quantise_h(c, h_bf):
-            nc.vector.quantize_mx(h_codes[c][:].bitcast(FP8X4), h_sc[c][:], h_bf[:].rearrange("p j t -> p (j t)"))
+        def quantise_h(c):
+            nc.vector.quantize_mx(h_codes[c].bitcast(FP8X4), h_sc[c][:], h_bf[c].rearrange("p j t -> p (j t)"))
 
-        wd_bf = x_pairs[0][:]
-
-        def round_wd():
-            nc.vector.tensor_copy(
-                wd_bf.rearrange("p (u m t) -> p m u t", u=PACK, t=PACK),
-                wd_raw[:].rearrange("p t (m u) -> p m u t", u=PACK),
-            )
-
-        y_banks = []
+        wd_bf = x_pairs[1][:]
+        wd_out = wd_bf.rearrange("p (u m t) -> p m u t", u=PACK, t=PACK)
+        wd_in = wd_raw[:].rearrange("p t (m u) -> p m u t", u=PACK)
 
         def second_layer(c):
             g, cols = divmod(c * CW, GW)[0], slice(c * CW % GW, c * CW % GW + CW)
@@ -216,13 +208,12 @@ def tile_list_htabg_glu_noneP_kernel(
                     y[:, u, :],
                     lhsT=wd_codes[:, P * u : P * (u + 1)].bitcast(FP8X4),
                     lhsT_scale=wd_sc[:, P * u : P * (u + 1)],
-                    rhs=h_codes[c][:].bitcast(FP8X4),
+                    rhs=h_codes[c].bitcast(FP8X4),
                     rhs_scale=h_sc[c][:],
                     start=True,
                     stop=True,
                 )
             nc.scalar.copy(y_f32[g][:, :, cols], y[:])
-            y_banks.append((y_bf[g][:, cols, :], y))
             if c % 2 == 1:
                 nc.sync.dma_start(out_rows[:, :, g * GW : (g + 1) * GW], y_f32[g][:])
 
@@ -242,36 +233,47 @@ def tile_list_htabg_glu_noneP_kernel(
         def store_words(queue, first, stop):
             queue.dma_start(out_words[:, first:stop], y_codes[:, first:stop])
 
-        prepare(0)
-        prepare(1)
-        prepare(2)
-        prepare(3)
-        round_wd()
+        for g in range(groups):
+            prepare(g)
+        quantise_x(0)
+        nc.vector.tensor_copy(x_bf[3][:, :, 2:4], picked_hi[:, :, 3 * GW : J].rearrange("p t j -> p j t"))
+        for g in range(1, groups):
+            quantise_x(g)
         for c in range(chunks):
             gate(c)
-        h_rounded = [first_layer(0)]
+        h_early = keep.tile([P, AHEAD, CW, PACK], BF16, name="h_early", align_bytes=64)
+        h_bf = [h_early[:, c] for c in range(AHEAD)]
+        first_layer(0)
+        nc.vector.tensor_copy(wd_out[:, 0:WD_VECTOR], wd_in[:, 0:WD_VECTOR])
+        nc.gpsimd.tensor_scalar(wd_out[:, WD_VECTOR:P], wd_in[:, WD_VECTOR:P], 1.0, 0.0, MULT, ADD)
+        for c in range(1, AHEAD):
+            first_layer(c)
         nc.vector.quantize_mx(wd_codes[:].bitcast(FP8X4), wd_sc[:], wd_bf)
-        whole, back_half = slice(0, GW), slice(CW, GW)
-        quantise_h(0, h_rounded[0])
-        second_layer(0)
-        h_rounded.append(first_layer(1))
-        for c in range(1, chunks):
-            if c + 1 < chunks - 1:
-                h_rounded.append(first_layer(c + 1))
-            quantise_h(c, h_rounded[c])
+        h_words = keep.tile([P, chunks, CW], U32, name="h_words", tag="wd_raw", align_bytes=64)
+        h_codes = [h_words[:, c, :] for c in range(chunks)]
+        h_late = keep.tile([P, chunks - AHEAD, CW, PACK], BF16, name="h_late", tag="x_pair1", align_bytes=64)
+        h_bf.extend(h_late[:, c] for c in range(chunks - AHEAD))
+        for c in range(AHEAD):
+            quantise_h(c)
             second_layer(c)
-            if c + 1 == chunks - 1:
-                h_rounded.append(first_layer(c + 1))
-        for c in SCALAR_CHUNKS:
-            rounded, bank = y_banks[c]
-            nc.scalar.copy(rounded, bank[:].rearrange("p t j -> p j t"))
+        first_layer(AHEAD)
+        for c in range(AHEAD + 1, chunks):
+            first_layer(c)
+            quantise_h(c - 1)
+            second_layer(c - 1)
+        quantise_h(chunks - 1)
+        second_layer(chunks - 1)
+        y_tile = keep.tile([P, J, PACK], BF16, name="y_tile", tag="gate7", align_bytes=64)
+        y_bf = [y_tile[:, g * GW : (g + 1) * GW, :] for g in range(groups)]
+        y_codes = keep.tile([P, J], I32, name="y_codes", align_bytes=64)
+        whole = slice(0, GW)
         round_y(0, whole)
         round_y(1, whole)
         quantise_y(0, whole)
+        round_y(2, whole)
         quantise_y(1, whole)
         store_words(nc.sync, 0, 2 * GW)
-        round_y(2, whole)
-        round_y(3, back_half)
+        round_y(3, whole)
         quantise_y(2, whole)
         quantise_y(3, whole)
         store_words(nc.scalar, 2 * GW, J)

@@ -23,7 +23,7 @@ PACK = 4
 GW = 256
 CW = 128
 SPARE = P - 16
-WD_VECTOR = 32
+WD_VECTOR = 48
 AHEAD = 4
 
 
@@ -114,11 +114,8 @@ def tile_list_htabg_glu_noneP_kernel(
                 nc.tensor.transpose(back[:, r, :], spread[:, r, :], ident[:])
             nc.scalar.copy(wgt[:, half * J // 2 : (half + 1) * J // 2], back[:].rearrange("p r c -> p (r c)"))
 
-        x_pairs = [keep.tile([P, 2 * GW * PACK], BF16, name="x_pair%d" % g, align_bytes=64) for g in range(groups // 2)]
-        x_bf = [
-            x_pairs[g // 2][:, g % 2 * GW * PACK : (g % 2 + 1) * GW * PACK].rearrange("p (j t) -> p j t", t=PACK)
-            for g in range(groups)
-        ]
+        x_all = keep.tile([P, J * PACK], BF16, name="x_all", align_bytes=64)
+        x_bf = [x_all[:, g * GW * PACK : (g + 1) * GW * PACK].rearrange("p (j t) -> p j t", t=PACK) for g in range(groups)]
         picked_lo = keep.tile([P, 2, J], F32, name="picked_lo")
         picked_hi = keep.tile([P, 2, J], F32, name="picked_hi", align_bytes=64)
         nc.vector.tensor_tensor(picked_lo[:, 0, :], x_planes[0][:].indirect(head_list[:]), wgt[:], MULT)
@@ -196,9 +193,11 @@ def tile_list_htabg_glu_noneP_kernel(
         def quantise_h(c):
             nc.vector.quantize_mx(h_codes[c].bitcast(FP8X4), h_sc[c][:], h_bf[c].rearrange("p j t -> p (j t)"))
 
-        wd_bf = x_pairs[1][:]
+        wd_bf = x_all[:, GW * PACK : 3 * GW * PACK]
         wd_out = wd_bf.rearrange("p (u m t) -> p m u t", u=PACK, t=PACK)
         wd_in = wd_raw[:].rearrange("p t (m u) -> p m u t", u=PACK)
+
+        y_banks = []
 
         def second_layer(c):
             g, cols = divmod(c * CW, GW)[0], slice(c * CW % GW, c * CW % GW + CW)
@@ -214,6 +213,7 @@ def tile_list_htabg_glu_noneP_kernel(
                     stop=True,
                 )
             nc.scalar.copy(y_f32[g][:, :, cols], y[:])
+            y_banks.append(y)
             if c % 2 == 1:
                 nc.sync.dma_start(out_rows[:, :, g * GW : (g + 1) * GW], y_f32[g][:])
 
@@ -243,15 +243,14 @@ def tile_list_htabg_glu_noneP_kernel(
             gate(c)
         h_early = keep.tile([P, AHEAD, CW, PACK], BF16, name="h_early", align_bytes=64)
         h_bf = [h_early[:, c] for c in range(AHEAD)]
-        first_layer(0)
         nc.vector.tensor_copy(wd_out[:, 0:WD_VECTOR], wd_in[:, 0:WD_VECTOR])
         nc.gpsimd.tensor_scalar(wd_out[:, WD_VECTOR:P], wd_in[:, WD_VECTOR:P], 1.0, 0.0, MULT, ADD)
-        for c in range(1, AHEAD):
+        for c in range(AHEAD):
             first_layer(c)
         nc.vector.quantize_mx(wd_codes[:].bitcast(FP8X4), wd_sc[:], wd_bf)
         h_words = keep.tile([P, chunks, CW], U32, name="h_words", tag="wd_raw", align_bytes=64)
         h_codes = [h_words[:, c, :] for c in range(chunks)]
-        h_late = keep.tile([P, chunks - AHEAD, CW, PACK], BF16, name="h_late", tag="x_pair1", align_bytes=64)
+        h_late = keep.tile([P, chunks - AHEAD, CW, PACK], BF16, name="h_late", tag="x_all", align_bytes=64)
         h_bf.extend(h_late[:, c] for c in range(chunks - AHEAD))
         for c in range(AHEAD):
             quantise_h(c)
@@ -263,17 +262,19 @@ def tile_list_htabg_glu_noneP_kernel(
             second_layer(c - 1)
         quantise_h(chunks - 1)
         second_layer(chunks - 1)
-        y_tile = keep.tile([P, J, PACK], BF16, name="y_tile", tag="gate7", align_bytes=64)
-        y_bf = [y_tile[:, g * GW : (g + 1) * GW, :] for g in range(groups)]
+        y_last = keep.tile([P, GW, PACK], BF16, name="y_last", tag="wd_raw", align_bytes=64)
+        y_tile = keep.tile([P, 3 * GW, PACK], BF16, name="y_tile", tag="gate7", align_bytes=64)
+        y_bf = [y_tile[:, g * GW : (g + 1) * GW, :] for g in range(3)] + [y_last[:]]
         y_codes = keep.tile([P, J], I32, name="y_codes", align_bytes=64)
         whole = slice(0, GW)
+        nc.scalar.copy(y_last[:, 0:CW, :], y_banks[chunks - 2][:].rearrange("p t j -> p j t"))
         round_y(0, whole)
         round_y(1, whole)
         quantise_y(0, whole)
         round_y(2, whole)
         quantise_y(1, whole)
         store_words(nc.sync, 0, 2 * GW)
-        round_y(3, whole)
+        round_y(3, slice(CW, GW))
         quantise_y(2, whole)
         quantise_y(3, whole)
         store_words(nc.scalar, 2 * GW, J)

@@ -42,20 +42,20 @@ def tile_list_htabg_glu_noneP_kernel(
         tab_list = keep.tile([P, J // 16], U16, name="tab_list")
         tab_sc = keep.tile([P, T], U8, name="tab_sc", align_bytes=64)
         w_sc_raw = keep.tile([P, 2 * R], U8, name="w_sc_raw", align_bytes=64)
-        nc.gpsimd.memset(tab_sc[0:SPARE, :].bitcast(I32), 0)
         ident = keep.tile([P, P], F32, name="ident")
-        ones = keep.tile([P, P], F32, name="ones")
-        column = keep.tile([P, P], F32, name="column", align_bytes=64)
-        row = keep.tile([P, P], F32, name="row", align_bytes=64)
+        ones = keep.tile([P, P - 32], F32, name="ones")
+        column = keep.tile([P, 32], F32, name="column", align_bytes=64)
+        row = keep.tile([P, 32], F32, name="row", align_bytes=64)
         nc.vector.memset(ones[:], 1.0)
-        nc.scalar.activation(ident[0:32, 32:P], ones[0:32, 32:P], SILU, scale=0.0)
+        nc.scalar.activation(ident[0:32, 32:P], ones[0:32, :], SILU, scale=0.0)
+        nc.vector.tensor_tensor_scan(column[:], ones[:, 0:32], ones[:, 0:32], 0.0, MULT, ADD)
+        nc.vector.memset(tab_sc[0:SPARE, :].bitcast(I32), 0)
+        nc.vector.transpose(row[:], column[:])
         nc.vector.memset(ident[32:64, :], 0.0)
         nc.vector.memset(ident[64:P, :], 0.0)
-        nc.vector.tensor_tensor_scan(column[:], ones[:], ones[:], 0.0, MULT, ADD)
-        nc.vector.transpose(row[:], column[:])
         for q in range(4):
             block = slice(32 * q, 32 * (q + 1))
-            nc.vector.tensor_tensor(ident[block, block], column[block, block], row[block, block], IS_EQUAL)
+            nc.vector.tensor_tensor(ident[block, block], column[block, :], row[block, :], IS_EQUAL)
 
         nc.vector.memset(w_sc_raw[:].bitcast(I32), 0)
         v_sc = keep.tile([P, J], U8, name="v_sc", align_bytes=64)

@@ -42,6 +42,7 @@ def tile_list_htabg_glu_noneP_kernel(
         tab_list = keep.tile([P, J // 16], U16, name="tab_list")
         tab_sc = keep.tile([P, T], U8, name="tab_sc", align_bytes=64)
         w_sc_raw = keep.tile([P, 2 * R], U8, name="w_sc_raw", align_bytes=64)
+        nc.gpsimd.memset(tab_sc[0:SPARE, :].bitcast(I32), 0)
         ident = keep.tile([P, P], F32, name="ident")
         ones = keep.tile([P, P - 32], F32, name="ones")
         column = keep.tile([P, 32], F32, name="column", align_bytes=64)
@@ -49,7 +50,6 @@ def tile_list_htabg_glu_noneP_kernel(
         nc.vector.memset(ones[:], 1.0)
         nc.scalar.activation(ident[0:32, 32:P], ones[0:32, :], SILU, scale=0.0)
         nc.vector.tensor_tensor_scan(column[:], ones[:, 0:32], ones[:, 0:32], 0.0, MULT, ADD)
-        nc.vector.memset(tab_sc[0:SPARE, :].bitcast(I32), 0)
         nc.vector.transpose(row[:], column[:])
         nc.vector.memset(ident[32:64, :], 0.0)
         nc.vector.memset(ident[64:P, :], 0.0)

@@ -23,7 +23,6 @@ PACK = 4
 GW = 256
 CW = 128
 SPARE = P - 16
-WD_VECTOR = 48
 AHEAD = 4
 
 
@@ -36,7 +35,14 @@ def tile_list_htabg_glu_noneP_kernel(
     chunks = J // CW
     with ExitStack() as ctx:
         keep = ctx.enter_context(tc.tile_pool(name="keep", bufs=1))
+        shared = ctx.enter_context(tc.tile_pool(name="shared", bufs=1))
         psum = ctx.enter_context(tc.psum_pool(name="psum", bufs=1))
+
+        def bank(index, name):
+            return psum.tile([P, PACK, CW], F32, name=name, tag="bank%d" % index)
+
+        def places(offsets, first, stop):
+            return offsets[:, first // 16 : stop // 16]
 
         head_list = keep.tile([P, J // 16], U16, name="head_list")
         tab_list = keep.tile([P, J // 16], U16, name="tab_list")
@@ -72,8 +78,6 @@ def tile_list_htabg_glu_noneP_kernel(
         x_planes = [keep.tile([P, T], F32, name="x_plane%d" % i) for i in range(PACK)]
         v_sc_spaced = keep.tile([P, J], U8, name="v_sc_spaced", align_bytes=64)
         nc.vector.tensor_copy(v_sc_spaced[:], tab_sc[:].indirect(tab_list[:]))
-        tab_w = keep.tile([P, T], I32, name="tab_w")
-        nc.sync.dma_start(tab_w[:], tab_words[0].rearrange("p t i -> p (t i)").bitcast(I32))
         nc.sync.dma_start(head_list[:], offs2)
         w_raw = [keep.tile([P, 2 * R], U8, name="w_raw%d" % a) for a in range(2)]
 
@@ -94,44 +98,44 @@ def tile_list_htabg_glu_noneP_kernel(
         for q in range(4):
             nc.sync.dma_start(v_sc[q:P:32, :].bitcast(I32), v_sc_spaced[SPARE + q : P : 4, :].bitcast(I32))
         nc.sync.dma_start(x_planes[3][:], x_rows[:, 3, :])
-        wd_raw = keep.tile([P, PACK, N], F32, name="wd_raw", align_bytes=64)
         wd_rows = wd.rearrange("(b t i) n -> t b i n", t=PACK, i=8)
-        for t in range(PACK):
-            nc.sync.dma_start(wd_raw[:, t, :], wd_rows[t])
+        wd_raw = [keep.tile([P, PACK, N // 2], F32, name="wd_raw%d" % half, align_bytes=64) for half in range(2)]
 
-        turned = psum.tile([P, PACK, CW], F32, name="turned", tag="ya_y", bufs=5)
+        def load_wd(half):
+            for t in range(PACK):
+                nc.sync.dma_start(wd_raw[half][:, t, :], wd_rows[t][:, :, half * N // 2 : (half + 1) * N // 2])
+
+        load_wd(0)
+        tab_w = keep.tile([P, T], I32, name="tab_w")
+        nc.sync.dma_start(tab_w[:], tab_words[0].rearrange("p t i -> p (t i)").bitcast(I32))
+        load_wd(1)
+
+        turned = bank(0, "turned")
         nc.tensor.transpose(turned[:, 0, :], wgt_rows[:], ident[:])
-        for half in range(2):
-            spread = keep.tile([P, PACK, P], F32, name="spread%d" % half, align_bytes=64)
+        for g in range(groups):
+            spread = keep.tile([P, 2, P], F32, name="spread%d" % g, align_bytes=64)
             nc.scalar.copy(
                 spread[:].rearrange("c r (g s e) -> c r g s e", s=2, e=8),
-                turned[:, 0, :].rearrange("c (s r g) -> c r g s", s=2, g=8)[:, PACK * half : PACK * (half + 1)]
+                turned[:, 0, :].rearrange("c (s r g) -> c r g s", s=2, g=8)[:, 2 * g : 2 * (g + 1)]
                 .unsqueeze(4)
-                .to_broadcast([P, PACK, 8, 2, 8]),
+                .to_broadcast([P, 2, 8, 2, 8]),
             )
-            back = psum.tile([P, PACK, CW], F32, name="back", tag="ya_y", bufs=5)
-            for r in range(PACK):
+            back = bank(1 + g, "back")
+            for r in range(2):
                 nc.tensor.transpose(back[:, r, :], spread[:, r, :], ident[:])
-            nc.scalar.copy(wgt[:, half * J // 2 : (half + 1) * J // 2], back[:].rearrange("p r c -> p (r c)"))
+            nc.scalar.copy(wgt[:, g * GW : (g + 1) * GW], back[:, 0:2, :].rearrange("p r c -> p (r c)"))
 
-        x_all = keep.tile([P, J * PACK], BF16, name="x_all", align_bytes=64)
-        x_bf = [x_all[:, g * GW * PACK : (g + 1) * GW * PACK].rearrange("p (j t) -> p j t", t=PACK) for g in range(groups)]
+        x_early = keep.tile([P, 2 * GW, PACK], BF16, name="x_early", align_bytes=64)
+        x_late = shared.tile([P, 2 * GW, PACK], BF16, name="x_late", align_bytes=64, offset=0)
+        x_bf = [tile[:, k * GW : (k + 1) * GW, :] for tile in (x_early, x_late) for k in range(2)]
         picked_lo = keep.tile([P, 2, J], F32, name="picked_lo")
         picked_hi = keep.tile([P, 2, J], F32, name="picked_hi", align_bytes=64)
-        nc.vector.tensor_tensor(picked_lo[:, 0, :], x_planes[0][:].indirect(head_list[:]), wgt[:], MULT)
-        for half in range(2):
-            cols = slice(half * J // 2, (half + 1) * J // 2)
-            nc.vector.tensor_tensor(
-                picked_lo[:, 1, cols], x_planes[1][:].indirect(head_list[:, cols.start // 16 : cols.stop // 16]), wgt[:, cols], MULT
-            )
-        for g in range(groups):
-            nc.scalar.copy(x_bf[g][:, :, 0:2], picked_lo[:, :, g * GW : (g + 1) * GW].rearrange("p t j -> p j t"))
-        v_codes = keep.tile([P, J], U32, name="v_codes", align_bytes=64)
-        nc.vector.tensor_copy(v_codes[:], tab_w[:].bitcast(U32).indirect(tab_list[:]))
 
-        nc.vector.tensor_tensor(picked_hi[:, 0, :], x_planes[2][:].indirect(head_list[:]), wgt[:], MULT)
+        def pick(picked, i, first, stop):
+            offsets = head_list[:] if stop - first == J else places(head_list, first, stop)
+            nc.vector.tensor_tensor(picked[:, i % 2, first:stop], x_planes[i][:].indirect(offsets), wgt[:, first:stop], MULT)
 
-        dealt = keep.tile([P, 6 * R], U8, name="dealt", tag="spread1", align_bytes=64)
+        dealt = keep.tile([P, 6 * R], U8, name="dealt", align_bytes=64)
         w_sc = dealt[:, 4 * R :]
         w_codes = dealt[:, : 4 * R].rearrange("p (a c) -> p a c", a=2)
         for a in range(2):
@@ -144,31 +148,35 @@ def tile_list_htabg_glu_noneP_kernel(
                 w_raw[a][:].bitcast(U32).rearrange("p (b t w) -> p t b w", t=PACK, w=4),
             )
 
+        for g in range(groups):
+            pick(picked_lo, 0, g * GW, (g + 1) * GW)
+        for half in range(2):
+            pick(picked_lo, 1, half * J // 2, (half + 1) * J // 2)
+        for g in range(groups):
+            nc.scalar.copy(x_bf[g][:, :, 0:2], picked_lo[:, :, g * GW : (g + 1) * GW].rearrange("p t j -> p j t"))
+        pick(picked_hi, 2, 0, J)
+
         x_codes = [keep.tile([P, GW], U32, name="x_codes%d" % g, align_bytes=64) for g in range(groups)]
         x_sc = [keep.tile([P, GW], U8, name="x_sc%d" % g, align_bytes=64) for g in range(groups)]
-        wd_codes = keep.tile([P, N], U32, name="wd_codes", align_bytes=64)
         wd_sc = keep.tile([P, N], U8, name="wd_sc", align_bytes=64)
         y_sc = keep.tile([P, J], U8, name="y_sc", align_bytes=64)
         y_f32 = [keep.tile([P, PACK, GW], F32, name="y_f32_%d" % g) for g in range(groups)]
         h_sc = [keep.tile([P, CW], U8, name="h_sc%d" % c, align_bytes=64) for c in range(chunks)]
+        gates = [keep.tile([P, CW, PACK], F32, name="gate%d" % c, align_bytes=64) for c in range(chunks)]
+        h_bf = []
         out_rows = out_0.rearrange("(p t) j -> p t j", t=PACK)
         out_words = out_1[0].rearrange("p j i -> p (j i)").bitcast(I32)
 
-        def prepare(g):
-            cols = slice(g * GW, (g + 1) * GW)
-            nc.vector.tensor_tensor(
-                picked_hi[:, 1, cols], x_planes[3][:].indirect(head_list[:, g * GW // 16 : (g + 1) * GW // 16]), wgt[:, cols], MULT
-            )
-            if g < groups - 1:
-                nc.scalar.copy(x_bf[g][:, :, 2:4], picked_hi[:, :, cols].rearrange("p t j -> p j t"))
+        def chunk_of(tiles, c):
+            return tiles[c // 2][:, c % 2 * CW : (c % 2 + 1) * CW]
 
         def quantise_x(g):
             nc.vector.quantize_mx(x_codes[g][:].bitcast(FP8X4), x_sc[g][:], x_bf[g].rearrange("p j t -> p (j t)"))
 
-        def product(bank, a, codes, scales):
+        def product(sums, a, codes, scales):
             for t in range(PACK):
                 nc.tensor.matmul_mx(
-                    bank[:, t, :],
+                    sums[:, t, :],
                     lhsT=w_codes[:, a, 2 * P * t : 2 * P * (t + 1)].bitcast(FP4X4),
                     lhsT_scale=w_sc[:, a * R + P * t : a * R + P * (t + 1)],
                     rhs=codes.bitcast(FP8X4),
@@ -177,31 +185,38 @@ def tile_list_htabg_glu_noneP_kernel(
                     stop=True,
                 )
 
-        gates = [keep.tile([P, CW, PACK], F32, name="gate%d" % c, align_bytes=64) for c in range(chunks)]
-
         def gate(c):
-            g, cols = divmod(c * CW, GW)[0], slice(c * CW % GW, c * CW % GW + CW)
-            ya = psum.tile([P, PACK, CW], F32, name="ya", tag="ya_y", bufs=5)
-            product(ya, 0, x_codes[g][:, cols], x_sc[g][:, cols])
+            ya = bank(c, "ya")
+            product(ya, 0, chunk_of(x_codes, c), chunk_of(x_sc, c))
             nc.scalar.activation(gates[c][:], ya[:].rearrange("p t j -> p j t"), SILU)
 
-        def first_layer(c):
-            yb = psum.tile([P, PACK, CW], F32, name="yb", bufs=3)
-            product(yb, 1, v_codes[:, c * CW : (c + 1) * CW], v_sc[:, c * CW : (c + 1) * CW])
-            nc.vector.tensor_tensor(h_bf[c], yb[:].rearrange("p t j -> p j t"), gates[c][:], MULT)
+        v_codes = []
+        yb_banks = []
 
-        def quantise_h(c):
-            nc.vector.quantize_mx(h_codes[c].bitcast(FP8X4), h_sc[c][:], h_bf[c].rearrange("p j t -> p (j t)"))
+        def look_up(first, stop):
+            width = (stop - first) * CW
+            if first == 1:
+                words = keep.tile([P, width], U32, name="v_codes%d" % first, align_bytes=64)
+            else:
+                words = shared.tile([P, width], U32, name="v_codes%d" % first, align_bytes=64, offset=(4096 if first == 0 else 3072 + 4 * CW * (first % AHEAD)))
+            v_codes.extend(words[:, c * CW : (c + 1) * CW] for c in range(stop - first))
+            nc.vector.tensor_copy(words[:], tab_w[:].bitcast(U32).indirect(places(tab_list, first * CW, stop * CW)))
 
-        wd_bf = x_all[:, GW * PACK : 3 * GW * PACK]
-        wd_out = wd_bf.rearrange("p (u m t) -> p m u t", u=PACK, t=PACK)
-        wd_in = wd_raw[:].rearrange("p t (m u) -> p m u t", u=PACK)
+        def table_product(c, index):
+            yb = bank(index, "yb")
+            yb_banks.append(yb)
+            product(yb, 1, v_codes[c], v_sc[:, c * CW : (c + 1) * CW])
+
+        def gate_product(c):
+            h = keep.tile([P, CW, PACK], BF16, name="h_bf%d" % c, align_bytes=64)
+            h_bf.append(h)
+            nc.vector.tensor_tensor(h_bf[c][:], yb_banks[c][:].rearrange("p t j -> p j t"), gates[c][:], MULT)
 
         y_banks = []
 
-        def second_layer(c):
-            g, cols = divmod(c * CW, GW)[0], slice(c * CW % GW, c * CW % GW + CW)
-            y = psum.tile([P, PACK, CW], F32, name="y", tag="ya_y", bufs=5)
+        def second_layer(c, index):
+            nc.vector.quantize_mx(h_codes[c].bitcast(FP8X4), h_sc[c][:], h_bf[c][:].rearrange("p j t -> p (j t)"))
+            y = bank(index, "y")
             for u in range(PACK):
                 nc.tensor.matmul_mx(
                     y[:, u, :],
@@ -212,10 +227,14 @@ def tile_list_htabg_glu_noneP_kernel(
                     start=True,
                     stop=True,
                 )
-            nc.scalar.copy(y_f32[g][:, :, cols], y[:])
+            g = c // 2
+            nc.scalar.copy(y_f32[g][:, :, c % 2 * CW : (c % 2 + 1) * CW], y[:])
             y_banks.append(y)
             if c % 2 == 1:
                 nc.sync.dma_start(out_rows[:, :, g * GW : (g + 1) * GW], y_f32[g][:])
+
+        def round_from_bank(target, c):
+            nc.scalar.copy(target, y_banks[c][:].rearrange("p t j -> p j t"))
 
         def round_y(g, cols):
             nc.vector.tensor_copy(
@@ -223,60 +242,76 @@ def tile_list_htabg_glu_noneP_kernel(
                 y_f32[g][:, :, cols].rearrange("p t (c i) -> p c t i", i=4),
             )
 
-        def quantise_y(g, cols):
+        def quantise_y(g):
             nc.vector.quantize_mx(
-                y_codes[:, g * GW + cols.start : g * GW + cols.stop].bitcast(FP8X4),
-                y_sc[:, g * GW + cols.start : g * GW + cols.stop],
-                y_bf[g][:, cols, :].rearrange("p j t -> p (j t)"),
+                y_codes[:, g * GW : (g + 1) * GW].bitcast(FP8X4),
+                y_sc[:, g * GW : (g + 1) * GW],
+                y_bf[g].rearrange("p j t -> p (j t)"),
             )
 
         def store_words(queue, first, stop):
             queue.dma_start(out_words[:, first:stop], y_codes[:, first:stop])
 
         for g in range(groups):
-            prepare(g)
-        quantise_x(0)
+            cols = slice(g * GW, (g + 1) * GW)
+            pick(picked_hi, 3, cols.start, cols.stop)
+            if g < groups - 1:
+                nc.scalar.copy(x_bf[g][:, :, 2:4], picked_hi[:, :, cols].rearrange("p t j -> p j t"))
         nc.vector.tensor_copy(x_bf[3][:, :, 2:4], picked_hi[:, :, 3 * GW : J].rearrange("p t j -> p j t"))
-        for g in range(1, groups):
+        for g in range(groups):
             quantise_x(g)
-        for c in range(chunks):
+        wd_in = [raw[:].rearrange("p t (m u) -> p m u t", u=PACK) for raw in wd_raw]
+        wd_early = keep.tile([P, PACK, P // 2, PACK], BF16, name="wd_early", align_bytes=64)
+        nc.scalar.copy(wd_early[:].rearrange("p u m t -> p m u t"), wd_in[0])
+        for c in range(AHEAD):
             gate(c)
-        h_early = keep.tile([P, AHEAD, CW, PACK], BF16, name="h_early", align_bytes=64)
-        h_bf = [h_early[:, c] for c in range(AHEAD)]
-        nc.vector.tensor_copy(wd_out[:, 0:WD_VECTOR], wd_in[:, 0:WD_VECTOR])
-        nc.gpsimd.tensor_scalar(wd_out[:, WD_VECTOR:P], wd_in[:, WD_VECTOR:P], 1.0, 0.0, MULT, ADD)
+        look_up(0, 1)
+        look_up(1, AHEAD)
         for c in range(AHEAD):
-            first_layer(c)
-        nc.vector.quantize_mx(wd_codes[:].bitcast(FP8X4), wd_sc[:], wd_bf)
-        h_words = keep.tile([P, chunks, CW], U32, name="h_words", tag="wd_raw", align_bytes=64)
+            table_product(c, AHEAD + c)
+        wd_late = shared.tile([P, PACK, P // 2, PACK], BF16, name="wd_late", align_bytes=64, offset=3072)
+        nc.gpsimd.tensor_scalar(wd_late[:].rearrange("p u m t -> p m u t"), wd_in[1], 1.0, 0.0, MULT, ADD)
+        for c in range(AHEAD):
+            gate_product(c)
+            gate(AHEAD + c)
+        wd_codes = keep.tile([P, N], U32, name="wd_codes", tag="gate2", align_bytes=64)
+        for half, rounded in enumerate((wd_early, wd_late)):
+            for u in range(PACK):
+                cols = slice(P * u + half * P // 2, P * u + (half + 1) * P // 2)
+                nc.vector.quantize_mx(wd_codes[:, cols].bitcast(FP8X4), wd_sc[:, cols], rounded[:, u].rearrange("p m t -> p (m t)"))
+        h_words = keep.tile([P, chunks, CW], U32, name="h_words", tag="wd_raw1", align_bytes=64)
         h_codes = [h_words[:, c, :] for c in range(chunks)]
-        h_late = keep.tile([P, chunks - AHEAD, CW, PACK], BF16, name="h_late", tag="x_all", align_bytes=64)
-        h_bf.extend(h_late[:, c] for c in range(chunks - AHEAD))
         for c in range(AHEAD):
-            quantise_h(c)
-            second_layer(c)
-        first_layer(AHEAD)
-        for c in range(AHEAD + 1, chunks):
-            first_layer(c)
-            quantise_h(c - 1)
-            second_layer(c - 1)
-        quantise_h(chunks - 1)
-        second_layer(chunks - 1)
-        y_last = keep.tile([P, GW, PACK], BF16, name="y_last", tag="wd_raw", align_bytes=64)
-        y_tile = keep.tile([P, 3 * GW, PACK], BF16, name="y_tile", tag="gate7", align_bytes=64)
-        y_bf = [y_tile[:, g * GW : (g + 1) * GW, :] for g in range(3)] + [y_last[:]]
-        y_codes = keep.tile([P, J], I32, name="y_codes", align_bytes=64)
+            second_layer(c, c)
+        y_mid = keep.tile([P, GW, PACK], BF16, name="y_mid", align_bytes=64)
+        round_from_bank(y_mid[:, 0:CW, :], 2)
+        round_from_bank(y_mid[:, CW:GW, :], 3)
+        look_up(AHEAD, AHEAD + 1)
+        look_up(AHEAD + 1, chunks)
+        for c in range(AHEAD, chunks):
+            table_product(c, c)
+        gate_product(4)
+        gate_product(5)
+        second_layer(4, 0)
+        gate_product(6)
+        second_layer(5, 1)
+        gate_product(7)
+        second_layer(6, 2)
+        second_layer(7, 3)
+        y_last = keep.tile([P, GW, PACK], BF16, name="y_last", tag="wd_raw1", align_bytes=64)
+        y_tile = keep.tile([P, 2 * GW, PACK], BF16, name="y_tile", tag="gate7", align_bytes=64)
+        y_bf = [y_tile[:, 0:GW, :], y_mid[:], y_tile[:, GW : 2 * GW, :], y_last[:]]
+        y_codes = keep.tile([P, J], I32, name="y_codes", tag="h_bf7", align_bytes=64)
         whole = slice(0, GW)
-        nc.scalar.copy(y_last[:, 0:CW, :], y_banks[chunks - 2][:].rearrange("p t j -> p j t"))
+        round_from_bank(y_last[:, 0:CW, :], 6)
         round_y(0, whole)
-        round_y(1, whole)
-        quantise_y(0, whole)
+        quantise_y(1)
+        quantise_y(0)
         round_y(2, whole)
-        quantise_y(1, whole)
         store_words(nc.sync, 0, 2 * GW)
         round_y(3, slice(CW, GW))
-        quantise_y(2, whole)
-        quantise_y(3, whole)
+        quantise_y(2)
+        quantise_y(3)
         store_words(nc.scalar, 2 * GW, J)
         for q in range(4):
             queue = nc.sync if q % 2 == 0 else nc.scalar

@@ -126,14 +126,14 @@ def tile_list_htabg_glu_noneP_kernel(
             nc.scalar.copy(wgt[:, g * GW : (g + 1) * GW], back[:, 0:2, :].rearrange("p r c -> p (r c)"))
 
         x_early = keep.tile([P, 2 * GW, PACK], BF16, name="x_early", align_bytes=64)
-        x_late = shared.tile([P, 2 * GW, PACK], BF16, name="x_late", align_bytes=64, offset=0)
+        x_late = shared.tile([P, 2 * GW, PACK], BF16, name="x_late", align_bytes=64, offset=512)
         x_bf = [tile[:, k * GW : (k + 1) * GW, :] for tile in (x_early, x_late) for k in range(2)]
         picked_lo = keep.tile([P, 2, J], F32, name="picked_lo")
         picked_hi = keep.tile([P, 2, J], F32, name="picked_hi", align_bytes=64)
 
-        def pick(picked, i, first, stop):
+        def pick(target, i, first, stop):
             offsets = head_list[:] if stop - first == J else places(head_list, first, stop)
-            nc.vector.tensor_tensor(picked[:, i % 2, first:stop], x_planes[i][:].indirect(offsets), wgt[:, first:stop], MULT)
+            nc.vector.tensor_tensor(target, x_planes[i][:].indirect(offsets), wgt[:, first:stop], MULT)
 
         dealt = keep.tile([P, 6 * R], U8, name="dealt", align_bytes=64)
         w_sc = dealt[:, 4 * R :]
@@ -149,12 +149,12 @@ def tile_list_htabg_glu_noneP_kernel(
             )
 
         for g in range(groups):
-            pick(picked_lo, 0, g * GW, (g + 1) * GW)
+            pick(picked_lo[:, 0, g * GW : (g + 1) * GW], 0, g * GW, (g + 1) * GW)
         for half in range(2):
-            pick(picked_lo, 1, half * J // 2, (half + 1) * J // 2)
+            pick(picked_lo[:, 1, half * J // 2 : (half + 1) * J // 2], 1, half * J // 2, (half + 1) * J // 2)
         for g in range(groups):
             nc.scalar.copy(x_bf[g][:, :, 0:2], picked_lo[:, :, g * GW : (g + 1) * GW].rearrange("p t j -> p j t"))
-        pick(picked_hi, 2, 0, J)
+        pick(picked_hi[:, 0, :], 2, 0, J)
 
         x_codes = [keep.tile([P, GW], U32, name="x_codes%d" % g, align_bytes=64) for g in range(groups)]
         x_sc = [keep.tile([P, GW], U8, name="x_sc%d" % g, align_bytes=64) for g in range(groups)]
@@ -162,7 +162,7 @@ def tile_list_htabg_glu_noneP_kernel(
         y_sc = keep.tile([P, J], U8, name="y_sc", align_bytes=64)
         y_f32 = [keep.tile([P, PACK, GW], F32, name="y_f32_%d" % g) for g in range(groups)]
         h_sc = [keep.tile([P, CW], U8, name="h_sc%d" % c, align_bytes=64) for c in range(chunks)]
-        gates = [keep.tile([P, CW, PACK], F32, name="gate%d" % c, align_bytes=64) for c in range(chunks)]
+        gates = []
         h_bf = []
         out_rows = out_0.rearrange("(p t) j -> p t j", t=PACK)
         out_words = out_1[0].rearrange("p j i -> p (j i)").bitcast(I32)
@@ -188,6 +188,7 @@ def tile_list_htabg_glu_noneP_kernel(
         def gate(c):
             ya = bank(c, "ya")
             product(ya, 0, chunk_of(x_codes, c), chunk_of(x_sc, c))
+            gates.append(keep.tile([P, CW, PACK], F32, name="gate%d" % c, align_bytes=64))
             nc.scalar.activation(gates[c][:], ya[:].rearrange("p t j -> p j t"), SILU)
 
         v_codes = []
@@ -198,7 +199,7 @@ def tile_list_htabg_glu_noneP_kernel(
             if first == 1:
                 words = keep.tile([P, width], U32, name="v_codes%d" % first, align_bytes=64)
             else:
-                words = shared.tile([P, width], U32, name="v_codes%d" % first, align_bytes=64, offset=(4096 if first == 0 else 3072 + 4 * CW * (first % AHEAD)))
+                words = shared.tile([P, width], U32, name="v_codes%d" % first, align_bytes=64, offset=4 * CW * (first % AHEAD))
             v_codes.extend(words[:, c * CW : (c + 1) * CW] for c in range(stop - first))
             nc.vector.tensor_copy(words[:], tab_w[:].bitcast(U32).indirect(places(tab_list, first * CW, stop * CW)))
 
@@ -252,14 +253,17 @@ def tile_list_htabg_glu_noneP_kernel(
         def store_words(queue, first, stop):
             queue.dma_start(out_words[:, first:stop], y_codes[:, first:stop])
 
-        for g in range(groups):
+        for g in range(groups - 1):
             cols = slice(g * GW, (g + 1) * GW)
-            pick(picked_hi, 3, cols.start, cols.stop)
-            if g < groups - 1:
-                nc.scalar.copy(x_bf[g][:, :, 2:4], picked_hi[:, :, cols].rearrange("p t j -> p j t"))
-        nc.vector.tensor_copy(x_bf[3][:, :, 2:4], picked_hi[:, :, 3 * GW : J].rearrange("p t j -> p j t"))
-        for g in range(groups):
-            quantise_x(g)
+            pick(picked_hi[:, 1, cols], 3, cols.start, cols.stop)
+            nc.scalar.copy(x_bf[g][:, :, 2:4], picked_hi[:, :, cols].rearrange("p t j -> p j t"))
+        quantise_x(0)
+        pick(picked_hi[:, 1, 0:GW], 3, J - GW, J)
+        quantise_x(1)
+        last_pair = picked_hi[:].rearrange("p t j -> p (t j)")[:, J - GW : J + GW]
+        nc.vector.tensor_copy(x_bf[3][:, :, 2:4], last_pair.rearrange("p (t j) -> p j t", t=2))
+        quantise_x(2)
+        quantise_x(3)
         wd_in = [raw[:].rearrange("p t (m u) -> p m u t", u=PACK) for raw in wd_raw]
         wd_early = keep.tile([P, PACK, P // 2, PACK], BF16, name="wd_early", align_bytes=64)
         nc.scalar.copy(wd_early[:].rearrange("p u m t -> p m u t"), wd_in[0])
@@ -269,9 +273,9 @@ def tile_list_htabg_glu_noneP_kernel(
         look_up(1, AHEAD)
         for c in range(AHEAD):
             table_product(c, AHEAD + c)
-        wd_late = shared.tile([P, PACK, P // 2, PACK], BF16, name="wd_late", align_bytes=64, offset=3072)
+        wd_late = shared.tile([P, PACK, P // 2, PACK], BF16, name="wd_late", align_bytes=64, offset=0)
         nc.gpsimd.tensor_scalar(wd_late[:].rearrange("p u m t -> p m u t"), wd_in[1], 1.0, 0.0, MULT, ADD)
-        for c in range(AHEAD):
+        for c in range(AHEAD - 1):
             gate_product(c)
             gate(AHEAD + c)
         wd_codes = keep.tile([P, N], U32, name="wd_codes", tag="gate2", align_bytes=64)
@@ -281,23 +285,28 @@ def tile_list_htabg_glu_noneP_kernel(
                 nc.vector.quantize_mx(wd_codes[:, cols].bitcast(FP8X4), wd_sc[:, cols], rounded[:, u].rearrange("p m t -> p (m t)"))
         h_words = keep.tile([P, chunks, CW], U32, name="h_words", tag="wd_raw1", align_bytes=64)
         h_codes = [h_words[:, c, :] for c in range(chunks)]
-        for c in range(AHEAD):
-            second_layer(c, c)
+        second_layer(0, 0)
+        second_layer(1, 1)
+        look_up(4, 6)
+        table_product(4, 4)
+        second_layer(2, 2)
+        gate_product(3)
+        gate(7)
+        table_product(5, 5)
+        gate_product(4)
+        second_layer(3, 3)
         y_mid = keep.tile([P, GW, PACK], BF16, name="y_mid", align_bytes=64)
         round_from_bank(y_mid[:, 0:CW, :], 2)
-        round_from_bank(y_mid[:, CW:GW, :], 3)
-        look_up(AHEAD, AHEAD + 1)
-        look_up(AHEAD + 1, chunks)
-        for c in range(AHEAD, chunks):
-            table_product(c, c)
-        gate_product(4)
         gate_product(5)
         second_layer(4, 0)
-        gate_product(6)
+        look_up(6, chunks)
+        table_product(6, 6)
         second_layer(5, 1)
+        table_product(7, 7)
+        gate_product(6)
         gate_product(7)
-        second_layer(6, 2)
-        second_layer(7, 3)
+        second_layer(6, 3)
+        second_layer(7, 4)
         y_last = keep.tile([P, GW, PACK], BF16, name="y_last", tag="wd_raw1", align_bytes=64)
         y_tile = keep.tile([P, 2 * GW, PACK], BF16, name="y_tile", tag="gate7", align_bytes=64)
         y_bf = [y_tile[:, 0:GW, :], y_mid[:], y_tile[:, GW : 2 * GW, :], y_last[:]]
@@ -305,9 +314,10 @@ def tile_list_htabg_glu_noneP_kernel(
         whole = slice(0, GW)
         round_from_bank(y_last[:, 0:CW, :], 6)
         round_y(0, whole)
-        quantise_y(1)
+        round_y(1, slice(CW, GW))
         quantise_y(0)
         round_y(2, whole)
+        quantise_y(1)
         store_words(nc.sync, 0, 2 * GW)
         round_y(3, slice(CW, GW))
         quantise_y(2)

@@ -99,15 +99,18 @@ def tile_list_htabg_glu_noneP_kernel(
             nc.sync.dma_start(v_sc[q:P:32, :].bitcast(I32), v_sc_spaced[SPARE + q : P : 4, :].bitcast(I32))
         nc.sync.dma_start(x_planes[3][:], x_rows[:, 3, :])
         wd_rows = wd.rearrange("(b t i) n -> t b i n", t=PACK, i=8)
-        wd_raw = [keep.tile([P, PACK, N // 2], F32, name="wd_raw%d" % half, align_bytes=64) for half in range(2)]
+        wd_raw = [
+            shared.tile([P, PACK, N // 2], F32, name="wd_raw0", align_bytes=64, offset=8192),
+            keep.tile([P, PACK, N // 2], F32, name="wd_raw1", align_bytes=64),
+        ]
 
         def load_wd(half):
             for t in range(PACK):
                 nc.sync.dma_start(wd_raw[half][:, t, :], wd_rows[t][:, :, half * N // 2 : (half + 1) * N // 2])
 
-        load_wd(0)
         tab_w = keep.tile([P, T], I32, name="tab_w")
         nc.sync.dma_start(tab_w[:], tab_words[0].rearrange("p t i -> p (t i)").bitcast(I32))
+        load_wd(0)
         load_wd(1)
 
         turned = bank(0, "turned")
@@ -156,7 +159,7 @@ def tile_list_htabg_glu_noneP_kernel(
             nc.scalar.copy(x_bf[g][:, :, 0:2], picked_lo[:, :, g * GW : (g + 1) * GW].rearrange("p t j -> p j t"))
         pick(picked_hi[:, 0, :], 2, 0, J)
 
-        x_codes = [keep.tile([P, GW], U32, name="x_codes%d" % g, align_bytes=64) for g in range(groups)]
+        x_codes = []
         x_sc = [keep.tile([P, GW], U8, name="x_sc%d" % g, align_bytes=64) for g in range(groups)]
         wd_sc = keep.tile([P, N], U8, name="wd_sc", align_bytes=64)
         y_sc = keep.tile([P, J], U8, name="y_sc", align_bytes=64)
@@ -171,6 +174,10 @@ def tile_list_htabg_glu_noneP_kernel(
             return tiles[c // 2][:, c % 2 * CW : (c % 2 + 1) * CW]
 
         def quantise_x(g):
+            if g < 2:
+                x_codes.append(keep.tile([P, GW], U32, name="x_codes%d" % g, align_bytes=64))
+            else:
+                x_codes.append(shared.tile([P, GW], U32, name="x_codes%d" % g, align_bytes=64, offset=4864 + 1024 * (g - 2)))
             nc.vector.quantize_mx(x_codes[g][:].bitcast(FP8X4), x_sc[g][:], x_bf[g].rearrange("p j t -> p (j t)"))
 
         def product(sums, a, codes, scales):
@@ -188,7 +195,10 @@ def tile_list_htabg_glu_noneP_kernel(
         def gate(c):
             ya = bank(c, "ya")
             product(ya, 0, chunk_of(x_codes, c), chunk_of(x_sc, c))
-            gates.append(keep.tile([P, CW, PACK], F32, name="gate%d" % c, align_bytes=64))
+            if c in (AHEAD, AHEAD + 1, AHEAD + 2):
+                gates.append(shared.tile([P, CW, PACK], F32, name="gate%d" % c, align_bytes=64, offset=8192 - 1024 + 2048 * (c - AHEAD)))
+            else:
+                gates.append(keep.tile([P, CW, PACK], F32, name="gate%d" % c, align_bytes=64))
             nc.scalar.activation(gates[c][:], ya[:].rearrange("p t j -> p j t"), SILU)
 
         v_codes = []
@@ -199,7 +209,7 @@ def tile_list_htabg_glu_noneP_kernel(
             if first == 1:
                 words = keep.tile([P, width], U32, name="v_codes%d" % first, align_bytes=64)
             else:
-                words = shared.tile([P, width], U32, name="v_codes%d" % first, align_bytes=64, offset=4 * CW * (first % AHEAD))
+                words = shared.tile([P, width], U32, name="v_codes%d" % first, align_bytes=64, offset=5632 if first == 0 else 512 + 4 * CW * (first % AHEAD))
             v_codes.extend(words[:, c * CW : (c + 1) * CW] for c in range(stop - first))
             nc.vector.tensor_copy(words[:], tab_w[:].bitcast(U32).indirect(places(tab_list, first * CW, stop * CW)))
 
@@ -262,18 +272,18 @@ def tile_list_htabg_glu_noneP_kernel(
         quantise_x(1)
         last_pair = picked_hi[:].rearrange("p t j -> p (t j)")[:, J - GW : J + GW]
         nc.vector.tensor_copy(x_bf[3][:, :, 2:4], last_pair.rearrange("p (t j) -> p j t", t=2))
-        quantise_x(2)
-        quantise_x(3)
         wd_in = [raw[:].rearrange("p t (m u) -> p m u t", u=PACK) for raw in wd_raw]
         wd_early = keep.tile([P, PACK, P // 2, PACK], BF16, name="wd_early", align_bytes=64)
-        nc.scalar.copy(wd_early[:].rearrange("p u m t -> p m u t"), wd_in[0])
         for c in range(AHEAD):
             gate(c)
+        nc.scalar.copy(wd_early[:].rearrange("p u m t -> p m u t"), wd_in[0])
         look_up(0, 1)
         look_up(1, AHEAD)
         for c in range(AHEAD):
             table_product(c, AHEAD + c)
-        wd_late = shared.tile([P, PACK, P // 2, PACK], BF16, name="wd_late", align_bytes=64, offset=0)
+        quantise_x(2)
+        quantise_x(3)
+        wd_late = shared.tile([P, PACK, P // 2, PACK], BF16, name="wd_late", align_bytes=64, offset=512)
         nc.gpsimd.tensor_scalar(wd_late[:].rearrange("p u m t -> p m u t"), wd_in[1], 1.0, 0.0, MULT, ADD)
         for c in range(AHEAD - 1):
             gate_product(c)

@@ -78,7 +78,6 @@ def tile_list_htabg_glu_noneP_kernel(
         x_planes = [keep.tile([P, T], F32, name="x_plane%d" % i) for i in range(PACK)]
         v_sc_spaced = keep.tile([P, J], U8, name="v_sc_spaced", align_bytes=64)
         nc.vector.tensor_copy(v_sc_spaced[:], tab_sc[:].indirect(tab_list[:]))
-        nc.sync.dma_start(head_list[:], offs2)
         w_raw = [keep.tile([P, 2 * R], U8, name="w_raw%d" % a) for a in range(2)]
 
         def load_scales(a, scales):
@@ -89,6 +88,7 @@ def tile_list_htabg_glu_noneP_kernel(
                 )
 
         nc.sync.dma_start(x_planes[0][:], x_rows[:, 0, :])
+        nc.sync.dma_start(head_list[:], offs2)
         load_scales(0, wa_scales)
         nc.sync.dma_start(w_raw[0][:].bitcast(I32), wa_words[0].bitcast(I32))
         nc.sync.dma_start(x_planes[1][:], x_rows[:, 1, :])
@@ -151,10 +151,9 @@ def tile_list_htabg_glu_noneP_kernel(
                 w_raw[a][:].bitcast(U32).rearrange("p (b t w) -> p t b w", t=PACK, w=4),
             )
 
-        for g in range(groups):
-            pick(picked_lo[:, 0, g * GW : (g + 1) * GW], 0, g * GW, (g + 1) * GW)
-        for half in range(2):
-            pick(picked_lo[:, 1, half * J // 2 : (half + 1) * J // 2], 1, half * J // 2, (half + 1) * J // 2)
+        for i, cuts in enumerate(((0, GW, 2 * GW, J), (0, 2 * GW, J))):
+            for first, stop in zip(cuts, cuts[1:]):
+                pick(picked_lo[:, i, first:stop], i, first, stop)
         for g in range(groups):
             nc.scalar.copy(x_bf[g][:, :, 0:2], picked_lo[:, :, g * GW : (g + 1) * GW].rearrange("p t j -> p j t"))
         pick(picked_hi[:, 0, :], 2, 0, J)
@@ -253,12 +252,9 @@ def tile_list_htabg_glu_noneP_kernel(
                 y_f32[g][:, :, cols].rearrange("p t (c i) -> p c t i", i=4),
             )
 
-        def quantise_y(g):
-            nc.vector.quantize_mx(
-                y_codes[:, g * GW : (g + 1) * GW].bitcast(FP8X4),
-                y_sc[:, g * GW : (g + 1) * GW],
-                y_bf[g].rearrange("p j t -> p (j t)"),
-            )
+        def quantise_y(rounded, first):
+            cols = slice(first, first + rounded.shape[1])
+            nc.vector.quantize_mx(y_codes[:, cols].bitcast(FP8X4), y_sc[:, cols], rounded.rearrange("p j t -> p (j t)"))
 
         def store_words(queue, first, stop):
             queue.dma_start(out_words[:, first:stop], y_codes[:, first:stop])
@@ -313,6 +309,10 @@ def tile_list_htabg_glu_noneP_kernel(
         table_product(6, 6)
         second_layer(5, 1)
         table_product(7, 7)
+        y_bf = {1: y_mid[:]}
+        round_y(1, slice(CW, GW))
+        y_first = keep.tile([P, CW, PACK], BF16, name="y_first", tag="h_bf5", align_bytes=64)
+        nc.gpsimd.tensor_scalar(y_first[:], y_f32[0][:, :, 0:CW].rearrange("p t j -> p j t"), 1.0, 0.0, MULT, ADD)
         gate_product(6)
         gate_product(7)
         second_layer(6, 3)
@@ -323,15 +323,15 @@ def tile_list_htabg_glu_noneP_kernel(
         y_codes = keep.tile([P, J], I32, name="y_codes", tag="h_bf7", align_bytes=64)
         whole = slice(0, GW)
         round_from_bank(y_last[:, 0:CW, :], 6)
-        round_y(0, whole)
-        round_y(1, slice(CW, GW))
-        quantise_y(0)
-        round_y(2, whole)
-        quantise_y(1)
+        round_y(0, slice(CW, GW))
+        quantise_y(y_first[:], 0)
+        quantise_y(y_bf[1], GW)
+        quantise_y(y_bf[0][:, CW:GW, :], CW)
         store_words(nc.sync, 0, 2 * GW)
+        round_y(2, whole)
         round_y(3, slice(CW, GW))
-        quantise_y(2)
-        quantise_y(3)
+        quantise_y(y_bf[2], 2 * GW)
+        quantise_y(y_bf[3], 3 * GW)
         store_words(nc.scalar, 2 * GW, J)
         for q in range(4):
             queue = nc.sync if q % 2 == 0 else nc.scalar

from contextlib import ExitStack

import concourse.mybir as mybir

K, L, R, N, T, J = 512, 512, 512, 512, 2048, 1024
FLOPS = 2 * J * (K * R + L * R + R * N)

F32 = mybir.dt.float32
BF16 = mybir.dt.bfloat16
I32 = mybir.dt.int32
U32 = mybir.dt.uint32
U16 = mybir.dt.uint16
U8 = mybir.dt.uint8
FP8X4 = mybir.dt.float8_e4m3fn_x4
FP4X4 = mybir.dt.float4_e2m1fn_x4
MULT = mybir.AluOpType.mult
ADD = mybir.AluOpType.add
IS_EQUAL = mybir.AluOpType.is_equal
SILU = mybir.ActivationFunctionType.Silu

P = 128
PACK = 4
GW = 256
CW = 128
SPARE = P - 16
AHEAD = 4


def tile_list_htabg_glu_noneP_kernel(
    tc, tab_words, tab_scales, xT, wgt2, wa_words, wa_scales, wb_words, wb_scales, wd, offs, offs2,
    out_0, out_1, out_2,
):
    nc = tc.nc
    groups = J // GW
    chunks = J // CW
    with ExitStack() as ctx:
        keep = ctx.enter_context(tc.tile_pool(name="keep", bufs=1))
        shared = ctx.enter_context(tc.tile_pool(name="shared", bufs=1))
        psum = ctx.enter_context(tc.psum_pool(name="psum", bufs=1))

        def bank(index, name):
            return psum.tile([P, PACK, CW], F32, name=name, tag="bank%d" % index)

        def places(offsets, first, stop):
            return offsets[:, first // 16 : stop // 16]

        head_list = keep.tile([P, J // 16], U16, name="head_list")
        tab_list = keep.tile([P, J // 16], U16, name="tab_list")
        tab_sc = keep.tile([P, T], U8, name="tab_sc", align_bytes=64)
        w_sc_raw = keep.tile([P, 2 * R], U8, name="w_sc_raw", align_bytes=64)
        nc.gpsimd.memset(tab_sc[0:SPARE, :].bitcast(I32), 0)
        ident = keep.tile([P, P], F32, name="ident")
        ones = keep.tile([P, P - 32], F32, name="ones")
        column = keep.tile([P, 32], F32, name="column", align_bytes=64)
        row = keep.tile([P, 32], F32, name="row", align_bytes=64)
        nc.vector.memset(ones[:], 1.0)
        nc.scalar.activation(ident[0:32, 32:P], ones[0:32, :], SILU, scale=0.0)
        nc.vector.tensor_tensor_scan(column[:], ones[:, 0:32], ones[:, 0:32], 0.0, MULT, ADD)
        nc.vector.transpose(row[:], column[:])
        nc.vector.memset(ident[32:64, :], 0.0)
        nc.vector.memset(ident[64:P, :], 0.0)
        for q in range(4):
            block = slice(32 * q, 32 * (q + 1))
            nc.vector.tensor_tensor(ident[block, block], column[block, :], row[block, :], IS_EQUAL)

        nc.vector.memset(w_sc_raw[:].bitcast(I32), 0)
        v_sc = keep.tile([P, J], U8, name="v_sc", align_bytes=64)
        nc.vector.memset(v_sc[:].bitcast(I32), 0)

        nc.sync.dma_start(tab_list[:], offs)
        nc.sync.dma_start(tab_sc[SPARE:P, :].bitcast(I32), tab_scales[0].bitcast(I32))
        wgt = keep.tile([P, J], F32, name="wgt")
        wgt_rows = keep.tile([P, P], F32, name="wgt_rows")
        nc.scalar.dma_start(
            wgt_rows[:], wgt2.rearrange("(g s) j -> g (s j)", s=16)[:, 0 : 2 * J].rearrange("g (m c) -> m g c", c=P)
        )
        x_rows = xT.rearrange("(p i) t -> p i t", i=PACK)
        x_planes = [keep.tile([P, T], F32, name="x_plane%d" % i) for i in range(PACK)]
        v_sc_spaced = keep.tile([P, J], U8, name="v_sc_spaced", align_bytes=64)
        nc.vector.tensor_copy(v_sc_spaced[:], tab_sc[:].indirect(tab_list[:]))
        w_raw = [keep.tile([P, 2 * R], U8, name="w_raw%d" % a) for a in range(2)]

        def load_scales(a, scales):
            for q in range(4):
                nc.sync.dma_start(
                    w_sc_raw[q:P:32, a * R : (a + 1) * R].bitcast(I32),
                    scales[0, q:16:4, :].bitcast(I32),
                )

        nc.sync.dma_start(x_planes[0][:], x_rows[:, 0, :])
        nc.sync.dma_start(head_list[:], offs2)
        load_scales(0, wa_scales)
        nc.sync.dma_start(w_raw[0][:].bitcast(I32), wa_words[0].bitcast(I32))
        nc.sync.dma_start(x_planes[1][:], x_rows[:, 1, :])
        nc.sync.dma_start(w_raw[1][:].bitcast(I32), wb_words[0].bitcast(I32))
        load_scales(1, wb_scales)
        nc.sync.dma_start(x_planes[2][:], x_rows[:, 2, :])
        for q in range(4):
            nc.sync.dma_start(v_sc[q:P:32, :].bitcast(I32), v_sc_spaced[SPARE + q : P : 4, :].bitcast(I32))
        nc.sync.dma_start(x_planes[3][:], x_rows[:, 3, :])
        wd_rows = wd.rearrange("(b t i) n -> t b i n", t=PACK, i=8)
        wd_raw = [
            shared.tile([P, PACK, N // 2], F32, name="wd_raw0", align_bytes=64, offset=8192),
            keep.tile([P, PACK, N // 2], F32, name="wd_raw1", align_bytes=64),
        ]

        def load_wd(half):
            for t in range(PACK):
                nc.sync.dma_start(wd_raw[half][:, t, :], wd_rows[t][:, :, half * N // 2 : (half + 1) * N // 2])

        tab_w = keep.tile([P, T], I32, name="tab_w")
        nc.sync.dma_start(tab_w[:], tab_words[0].rearrange("p t i -> p (t i)").bitcast(I32))
        load_wd(0)
        load_wd(1)

        turned = bank(0, "turned")
        nc.tensor.transpose(turned[:, 0, :], wgt_rows[:], ident[:])
        for g in range(groups):
            spread = keep.tile([P, 2, P], F32, name="spread%d" % g, align_bytes=64)
            nc.scalar.copy(
                spread[:].rearrange("c r (g s e) -> c r g s e", s=2, e=8),
                turned[:, 0, :].rearrange("c (s r g) -> c r g s", s=2, g=8)[:, 2 * g : 2 * (g + 1)]
                .unsqueeze(4)
                .to_broadcast([P, 2, 8, 2, 8]),
            )
            back = bank(1 + g, "back")
            for r in range(2):
                nc.tensor.transpose(back[:, r, :], spread[:, r, :], ident[:])
            nc.scalar.copy(wgt[:, g * GW : (g + 1) * GW], back[:, 0:2, :].rearrange("p r c -> p (r c)"))

        x_early = keep.tile([P, 2 * GW, PACK], BF16, name="x_early", align_bytes=64)
        x_late = shared.tile([P, 2 * GW, PACK], BF16, name="x_late", align_bytes=64, offset=512)
        x_bf = [tile[:, k * GW : (k + 1) * GW, :] for tile in (x_early, x_late) for k in range(2)]
        picked_lo = keep.tile([P, 2, J], F32, name="picked_lo")
        picked_hi = keep.tile([P, 2, J], F32, name="picked_hi", align_bytes=64)

        def pick(target, i, first, stop):
            offsets = head_list[:] if stop - first == J else places(head_list, first, stop)
            nc.vector.tensor_tensor(target, x_planes[i][:].indirect(offsets), wgt[:, first:stop], MULT)

        dealt = keep.tile([P, 6 * R], U8, name="dealt", align_bytes=64)
        w_sc = dealt[:, 4 * R :]
        w_codes = dealt[:, : 4 * R].rearrange("p (a c) -> p a c", a=2)
        for a in range(2):
            nc.scalar.copy(
                w_sc[:, a * R : (a + 1) * R].bitcast(U32).rearrange("p (t b w) -> p t b w", t=PACK, w=2),
                w_sc_raw[:, a * R : (a + 1) * R].bitcast(U32).rearrange("p (b t w) -> p t b w", t=PACK, w=2),
            )
            nc.scalar.copy(
                w_codes[:, a, :].bitcast(U32).rearrange("p (t b w) -> p t b w", t=PACK, w=4),
                w_raw[a][:].bitcast(U32).rearrange("p (b t w) -> p t b w", t=PACK, w=4),
            )

        for i, cuts in enumerate(((0, GW, 2 * GW, J), (0, 2 * GW, J))):
            for first, stop in zip(cuts, cuts[1:]):
                pick(picked_lo[:, i, first:stop], i, first, stop)
        for g in range(groups):
            nc.scalar.copy(x_bf[g][:, :, 0:2], picked_lo[:, :, g * GW : (g + 1) * GW].rearrange("p t j -> p j t"))
        pick(picked_hi[:, 0, :], 2, 0, J)

        x_codes = []
        x_sc = [keep.tile([P, GW], U8, name="x_sc%d" % g, align_bytes=64) for g in range(groups)]
        wd_sc = keep.tile([P, N], U8, name="wd_sc", align_bytes=64)
        y_sc = keep.tile([P, J], U8, name="y_sc", align_bytes=64)
        y_f32 = [keep.tile([P, PACK, GW], F32, name="y_f32_%d" % g) for g in range(groups)]
        h_sc = [keep.tile([P, CW], U8, name="h_sc%d" % c, align_bytes=64) for c in range(chunks)]
        gates = []
        h_bf = []
        out_rows = out_0.rearrange("(p t) j -> p t j", t=PACK)
        out_words = out_1[0].rearrange("p j i -> p (j i)").bitcast(I32)

        def chunk_of(tiles, c):
            return tiles[c // 2][:, c % 2 * CW : (c % 2 + 1) * CW]

        def quantise_x(g):
            if g < 2:
                x_codes.append(keep.tile([P, GW], U32, name="x_codes%d" % g, align_bytes=64))
            else:
                x_codes.append(shared.tile([P, GW], U32, name="x_codes%d" % g, align_bytes=64, offset=4864 + 1024 * (g - 2)))
            nc.vector.quantize_mx(x_codes[g][:].bitcast(FP8X4), x_sc[g][:], x_bf[g].rearrange("p j t -> p (j t)"))

        def product(sums, a, codes, scales):
            for t in range(PACK):
                nc.tensor.matmul_mx(
                    sums[:, t, :],
                    lhsT=w_codes[:, a, 2 * P * t : 2 * P * (t + 1)].bitcast(FP4X4),
                    lhsT_scale=w_sc[:, a * R + P * t : a * R + P * (t + 1)],
                    rhs=codes.bitcast(FP8X4),
                    rhs_scale=scales,
                    start=True,
                    stop=True,
                )

        def gate(c):
            ya = bank(c, "ya")
            product(ya, 0, chunk_of(x_codes, c), chunk_of(x_sc, c))
            if c in (AHEAD, AHEAD + 1, AHEAD + 2):
                gates.append(shared.tile([P, CW, PACK], F32, name="gate%d" % c, align_bytes=64, offset=8192 - 1024 + 2048 * (c - AHEAD)))
            else:
                gates.append(keep.tile([P, CW, PACK], F32, name="gate%d" % c, align_bytes=64))
            nc.scalar.activation(gates[c][:], ya[:].rearrange("p t j -> p j t"), SILU)

        v_codes = []
        yb_banks = []

        def look_up(first, stop):
            width = (stop - first) * CW
            if first == 1:
                words = keep.tile([P, width], U32, name="v_codes%d" % first, align_bytes=64)
            else:
                words = shared.tile([P, width], U32, name="v_codes%d" % first, align_bytes=64, offset=5632 if first == 0 else 512 + 4 * CW * (first % AHEAD))
            v_codes.extend(words[:, c * CW : (c + 1) * CW] for c in range(stop - first))
            nc.vector.tensor_copy(words[:], tab_w[:].bitcast(U32).indirect(places(tab_list, first * CW, stop * CW)))

        def table_product(c, index):
            yb = bank(index, "yb")
            yb_banks.append(yb)
            product(yb, 1, v_codes[c], v_sc[:, c * CW : (c + 1) * CW])

        def gate_product(c):
            h = keep.tile([P, CW, PACK], BF16, name="h_bf%d" % c, align_bytes=64)
            h_bf.append(h)
            nc.vector.tensor_tensor(h_bf[c][:], yb_banks[c][:].rearrange("p t j -> p j t"), gates[c][:], MULT)

        y_banks = []

        def second_layer(c, index):
            nc.vector.quantize_mx(h_codes[c].bitcast(FP8X4), h_sc[c][:], h_bf[c][:].rearrange("p j t -> p (j t)"))
            y = bank(index, "y")
            for u in range(PACK):
                nc.tensor.matmul_mx(
                    y[:, u, :],
                    lhsT=wd_codes[:, P * u : P * (u + 1)].bitcast(FP8X4),
                    lhsT_scale=wd_sc[:, P * u : P * (u + 1)],
                    rhs=h_codes[c].bitcast(FP8X4),
                    rhs_scale=h_sc[c][:],
                    start=True,
                    stop=True,
                )
            g = c // 2
            nc.scalar.copy(y_f32[g][:, :, c % 2 * CW : (c % 2 + 1) * CW], y[:])
            y_banks.append(y)
            if c % 2 == 1:
                nc.sync.dma_start(out_rows[:, :, g * GW : (g + 1) * GW], y_f32[g][:])

        def round_from_bank(target, c):
            nc.scalar.copy(target, y_banks[c][:].rearrange("p t j -> p j t"))

        def round_y(g, cols):
            nc.vector.tensor_copy(
                y_bf[g][:, cols, :].rearrange("p (c i) t -> p c t i", i=4),
                y_f32[g][:, :, cols].rearrange("p t (c i) -> p c t i", i=4),
            )

        def quantise_y(rounded, first):
            cols = slice(first, first + rounded.shape[1])
            nc.vector.quantize_mx(y_codes[:, cols].bitcast(FP8X4), y_sc[:, cols], rounded.rearrange("p j t -> p (j t)"))

        def store_words(queue, first, stop):
            queue.dma_start(out_words[:, first:stop], y_codes[:, first:stop])

        for g in range(groups - 1):
            cols = slice(g * GW, (g + 1) * GW)
            pick(picked_hi[:, 1, cols], 3, cols.start, cols.stop)
            nc.scalar.copy(x_bf[g][:, :, 2:4], picked_hi[:, :, cols].rearrange("p t j -> p j t"))
        quantise_x(0)
        pick(picked_hi[:, 1, 0:GW], 3, J - GW, J)
        quantise_x(1)
        last_pair = picked_hi[:].rearrange("p t j -> p (t j)")[:, J - GW : J + GW]
        nc.vector.tensor_copy(x_bf[3][:, :, 2:4], last_pair.rearrange("p (t j) -> p j t", t=2))
        wd_in = [raw[:].rearrange("p t (m u) -> p m u t", u=PACK) for raw in wd_raw]
        wd_early = keep.tile([P, PACK, P // 2, PACK], BF16, name="wd_early", align_bytes=64)
        for c in range(AHEAD):
            gate(c)
        nc.scalar.copy(wd_early[:].rearrange("p u m t -> p m u t"), wd_in[0])
        look_up(0, 1)
        look_up(1, AHEAD)
        for c in range(AHEAD):
            table_product(c, AHEAD + c)
        quantise_x(2)
        quantise_x(3)
        wd_late = shared.tile([P, PACK, P // 2, PACK], BF16, name="wd_late", align_bytes=64, offset=512)
        nc.gpsimd.tensor_scalar(wd_late[:].rearrange("p u m t -> p m u t"), wd_in[1], 1.0, 0.0, MULT, ADD)
        for c in range(AHEAD - 1):
            gate_product(c)
            gate(AHEAD + c)
        wd_codes = keep.tile([P, N], U32, name="wd_codes", tag="gate2", align_bytes=64)
        for half, rounded in enumerate((wd_early, wd_late)):
            for u in range(PACK):
                cols = slice(P * u + half * P // 2, P * u + (half + 1) * P // 2)
                nc.vector.quantize_mx(wd_codes[:, cols].bitcast(FP8X4), wd_sc[:, cols], rounded[:, u].rearrange("p m t -> p (m t)"))
        h_words = keep.tile([P, chunks, CW], U32, name="h_words", tag="wd_raw1", align_bytes=64)
        h_codes = [h_words[:, c, :] for c in range(chunks)]
        second_layer(0, 0)
        second_layer(1, 1)
        look_up(4, 6)
        table_product(4, 4)
        second_layer(2, 2)
        gate_product(3)
        gate(7)
        table_product(5, 5)
        gate_product(4)
        second_layer(3, 3)
        y_mid = keep.tile([P, GW, PACK], BF16, name="y_mid", align_bytes=64)
        round_from_bank(y_mid[:, 0:CW, :], 2)
        gate_product(5)
        second_layer(4, 0)
        look_up(6, chunks)
        table_product(6, 6)
        second_layer(5, 1)
        table_product(7, 7)
        y_bf = {1: y_mid[:]}
        round_y(1, slice(CW, GW))
        y_first = keep.tile([P, CW, PACK], BF16, name="y_first", tag="h_bf5", align_bytes=64)
        nc.gpsimd.tensor_scalar(y_first[:], y_f32[0][:, :, 0:CW].rearrange("p t j -> p j t"), 1.0, 0.0, MULT, ADD)
        gate_product(6)
        gate_product(7)
        second_layer(6, 3)
        second_layer(7, 4)
        y_last = keep.tile([P, GW, PACK], BF16, name="y_last", tag="wd_raw1", align_bytes=64)
        y_tile = keep.tile([P, 2 * GW, PACK], BF16, name="y_tile", tag="gate7", align_bytes=64)
        y_bf = [y_tile[:, 0:GW, :], y_mid[:], y_tile[:, GW : 2 * GW, :], y_last[:]]
        y_codes = keep.tile([P, J], I32, name="y_codes", tag="h_bf7", align_bytes=64)
        whole = slice(0, GW)
        round_from_bank(y_last[:, 0:CW, :], 6)
        round_y(0, slice(CW, GW))
        quantise_y(y_first[:], 0)
        quantise_y(y_bf[1], GW)
        quantise_y(y_bf[0][:, CW:GW, :], CW)
        store_words(nc.sync, 0, 2 * GW)
        round_y(2, whole)
        round_y(3, slice(CW, GW))
        quantise_y(y_bf[2], 2 * GW)
        quantise_y(y_bf[3], 3 * GW)
        store_words(nc.scalar, 2 * GW, J)
        for q in range(4):
            queue = nc.sync if q % 2 == 0 else nc.scalar
            queue.dma_start(out_2[0, q:16:4, :].bitcast(I32), y_sc[q:P:32, :].bitcast(I32))
